import numpy as np, ml_dtypes
CORES = [3,7,11,15,131,135,139,143]
N = 8
import mx_ref
BF = ml_dtypes.bfloat16
def gcols(t, e):
    v = np.concatenate([t.reshape(8, 16, -1, 4), np.zeros((8, 16, 1, 4), BF)], axis=2)
    return np.ascontiguousarray(np.stack([v[g][:, e[g]] for g in range(8)])).reshape(128, -1)
def tile(rs):
    return np.stack(rs, axis=2).reshape(128, -1).astype(BF)
def pick(q, e):
    c = np.concatenate([q[0].reshape(128, -1, 4), np.zeros((128, 1, 4), np.uint8)], axis=1); s = np.concatenate([q[1], np.ones((16, 1), np.uint8)], axis=1)
    return (np.ascontiguousarray(c[:, e].reshape(128, -1)), np.ascontiguousarray(s[:, e]))
def join(*qs):
    return (np.concatenate([q[0] for q in qs], axis=1), np.concatenate([q[1] for q in qs], axis=1))
def put(q, e, v):
    c, s = q[0].reshape(128, -1, 4).copy(), q[1].copy(); c[:, e] = v[0].reshape(128, -1, 4); s[:, e] = v[1]
    return (c.reshape(128, -1), s)
def pk(c, s):
    return (np.ascontiguousarray(c), mx_ref.live(s))
def emit(q):
    return q[0], q[1]
def packed(v, rng):
    q = [mx_ref.quantize(np.ascontiguousarray(v[r])) for r in range(N)]
    return np.stack([a for a, b in q]), np.stack([mx_ref.plane(b, rng) for a, b in q])
def values_of_codes():
    e, c = np.zeros((128, 128, 4), np.float32), np.zeros((128, 2, 4), np.uint8)
    e[np.arange(128), np.arange(128), 0] = 1
    c[:127, :, 0] = np.arange(256).reshape(2, 128).T[:127]
    return mx_ref.matmul(mx_ref.quantize(e.reshape(128, 512).astype(BF)), (c.reshape(128, 8), np.full((16, 2), 127, np.uint8))).T.reshape(-1).astype(np.float64)
CODE_VALUE, SCALE_VALUE = values_of_codes(), 2.0 ** (np.arange(256) - 127.0)
def decode(q):
    return (CODE_VALUE[q[0]].reshape(16, 8, -1, 4) * SCALE_VALUE[q[1]][:, None, :, None] + 0.0).reshape(128, -1).astype(np.float32)
def f(rng, *shape):
    return mx_ref.flush((rng.standard_normal(shape, dtype=np.float32) * np.exp2(rng.integers(-2, 3, shape[:-1] + (1,)))).astype(BF))
def wide(rng, *shape, cols=0):
    v = rng.standard_normal(shape, dtype=np.float32) * np.exp2(rng.integers(-12, 13, shape)).astype(np.float32)
    if cols: v *= np.repeat(np.exp2(rng.integers(-cols, cols + 1, shape[:-2] + (1, shape[-1] // 4))) * (rng.random(shape[:-2] + (1, shape[-1] // 4)) > 0.0625), 4, axis=-1).astype(np.float32)
    return mx_ref.flush(v.astype(BF))
C, B, F, K, R = 400, 80, 5, 64, 3
def order(p):
    return np.argsort(-(p[::16] + np.float32(0.0)), axis=1, kind="stable")
def layer(w, q):
    return tile([mx_ref.matmul(pick(w, np.arange(128 * b, 128 * b + 128)), q) * np.float32(0.03125) for b in range(4)])
def numbers_of(rng):
    return {"x": np.array(f(rng, N, 128, 4 * C)), "u": np.array(f(rng, N, 128, 512)), "v": np.array(f(rng, N, 128, 512))}
def weights(rng, w):
    c, p = packed(w, rng)
    return {"wc": c, "ws": p}
def still(rng, q=-1):
    w = np.zeros((N, 128, 4, 128, 4), np.float32)
    i = np.arange(128)
    c = np.where(rng.permutation(N) % 2 == 0, 32.0, -32.0)
    for b in range(4): w[:, i, b, i, b] = c[:, None]
    if q >= 0:
        for b in range(4):
            w[:, 16 * q, b, 16 * q, :] = 0
            w[:, 16 * q, b, 16 * q, (b + 1) % 4] = 32
    return weights(rng, w.reshape(N, 128, 2048).astype(BF))
def signs(rng):
    return np.stack([rng.permutation(8) % 2 * 2.0 - 1.0 for r in range(N)])
def planned(rng, kind):
    b = rng.permutation(F)
    n = np.zeros(F, int)
    if kind == 0: n[:] = B // F
    if kind == 1: n[b[0]] = B
    if kind == 2: n[b[:2]] = B // 2
    if kind == 3:
        n[min(b[:2])] = B // 2 - 1
        n[max(b[:2])] = B // 2
        n[b[2]] = 1
    e = rng.permutation(np.concatenate([B * i + rng.permutation(B)[:n[i]] for i in range(F)]))
    return np.concatenate([e, rng.permutation(np.setdiff1d(np.arange(C), e))])
def level(rng):
    a, n, block, may = np.zeros((C, 4)), np.zeros(C, int), np.arange(C) // B, list(range(F))
    for t in range(R):
        least, more = (C - B) // (F + t), (C - B) % (F + t)
        e = [int(j) for j in rng.permutation(may)]
        w = np.concatenate([rng.permutation(np.flatnonzero(block == e[i]))[least + int(i < more):] for i in range(F + t)])
        a[w, n[w]] = R - t
        n[w] += 1
        block[w] = F + 2 * t
        b = min(e[more:])
        s = np.flatnonzero(block == b)
        n[s] += 1
        block[s] = F + 2 * t + 1
        may = [j for j in may if j != b] + [F + 2 * t, F + 2 * t + 1]
    return a
def setup_inputs(rng):
    return {**numbers_of(rng), **weights(rng, f(rng, N, 128, 2048))}
def setup_inputs_ties(rng):
    d = numbers_of(rng)
    e = rng.permutation(N)
    x = d["x"].reshape(N, 8, 16, C, 4)
    for r in range(N):
        k = np.zeros(C, int) if r == e[0] else rng.permutation(C) % 5 // 2
        a = x[r][:, :8, :3].copy()
        a[:, :, 2] = 0
        x[r][:, :8] = a[:, :, k]
        if r == e[1]: x[r][:, :, k == 2] = 0
    u = d["u"].reshape(N, 8, 16, 128, 4)
    u[:, :, 8:, ::16] = 0
    w = np.array(f(rng, N, 128, 2048)).reshape(N, 8, 16, 4, 8, 16, 4)
    w[:, :, 8:, :, :, :8] = 0
    return {"x": x.reshape(N, 128, 4 * C), "u": u.reshape(N, 128, 512), "v": d["v"], **weights(rng, w.reshape(N, 128, 2048))}
def setup_inputs_blocks(rng):
    d = numbers_of(rng)
    x = d["x"].astype(np.float32).reshape(N, 8, 16, C, 4)
    o = rng.permutation(N)
    s = np.zeros((N, 8, C), int)
    for r in range(N):
        k = rng.permutation(8) % 4 if o[r] > 1 else np.full(8, o[r])
        for g in range(8): s[r, g, planned(rng, k[g])] = (C - 1 - np.arange(C)) // 2
    b = ((s[:, :, :, None] >> np.arange(8)) & 1) * np.exp2(np.arange(8) - 23.0)
    x[:, :, 0] = 0
    x[:, :, 0, :, 0] = signs(rng)[:, :, None]
    x[:, :, 8] = b[:, :, :, :4]
    x[:, :, 9] = b[:, :, :, 4:]
    x[:, :, 10:] = rng.integers(4, 8, (N, 8, 6, C, 4)) * rng.choice([-1.0, 1.0], (N, 8, 6, C, 4)) * 2.0 ** -20
    u = d["u"].reshape(N, 128, 128, 4)
    k = np.where(rng.permutation(N) < N // 2, 2.0 ** -30, 1.0).astype(np.float32).astype(BF)
    u[:, :, ::16] = 0
    for h in range(0, 128, 16):
        u[:, h, h, 0] = k
        u[:, h + 8:h + 10, h] = k[:, None, None]
    return {"x": x.reshape(N, 128, 4 * C).astype(BF), "u": u.reshape(N, 128, 512), "v": d["v"], **still(rng)}
def setup_inputs_sizes(rng):
    d = numbers_of(rng)
    x = d["x"].astype(np.float32).reshape(N, 8, 16, C, 4)
    a = rng.integers(-7, 8, (N, 8, C)) * 2.0 ** -30
    r, g = np.nonzero(signs(rng) > 0)
    a[r, g, rng.integers(0, C, len(r))] = 2.0 ** 30 * rng.choice([-1.0, 1.0], len(r))
    x[:, :, :8] = 0
    x[:, :, 0, :, 0] = a
    q = int(rng.integers(8))
    x[:, q, 0] = level(rng) * 2.0 ** -30
    u = d["u"].reshape(N, 128, 128, 4)
    k = signs(rng) * np.where(rng.permutation(N) < N // 2, 2.0 ** -30, 1.0)[:, None]
    k[:, q] = np.abs(k[:, q])
    u[:, :, ::16] = 0
    for h in range(8): u[:, 16 * h, 16 * h, 0] = k[:, h].astype(np.float32).astype(BF)
    return {"x": x.reshape(N, 128, 4 * C).astype(BF), "u": u.reshape(N, 128, 512), "v": d["v"], **still(rng, q)}
def setup_inputs_huge(rng):
    d = numbers_of(rng)
    x = 2.0 ** 30 * (0.6 + 0.4 * rng.random((N, 128, C, 4)))
    c = np.stack([rng.permutation(C) % 2 * 2.0 - 1.0 for r in range(N)])
    c[rng.permutation(N) < N // 2] = 1
    x *= c[:, None, :, None]
    u = d["u"].reshape(N, 128, 128, 4)
    a = 2.0 ** 30 * (1 - 0.25 * rng.random((N, 128, 8, 4))) * signs(rng)[:, None, :, None]
    u[:, :, ::16] = a.astype(np.float32).astype(BF)
    return {"x": x.astype(np.float32).reshape(N, 128, 4 * C).astype(BF), "u": u.reshape(N, 128, 512), "v": d["v"], **still(rng)}
def setup_inputs_spread(rng):
    d = setup_inputs(rng)
    d["x"] = wide(rng, N, 128, 4 * C, cols=6)
    return d
def check_inputs(d):
    b = []
    for k in ("x", "u", "v"):
        a = np.abs(d[k].astype(np.float32))
        if not (np.isfinite(a).all() and ((a == 0) | (a >= 2.0 ** -30) & (a <= 2.0 ** 30)).all()): b.append("a value of " + k)
    return b
def reference(x, u, v, wc, ws):
    qu = [mx_ref.quantize(u[r]) for r in range(N)]
    lay = [pk(wc[r], ws[r]) for r in range(N)]
    now = [x[r] for r in range(N)]
    block = np.tile(np.arange(C) // B, (N, 8, 1))
    gone = np.zeros((N, 8, F + 2 * R), bool)
    for t in range(R):
        first, made, stay, kept, sent = [], [], [], [], []
        for r in range(N):
            q = mx_ref.quantize(now[r])
            o = order(mx_ref.matmul(qu[r], q))
            first.append(o[:, :B])
            made.append(layer(lay[r], mx_ref.quantize(gcols(now[r], o[:, :B]))))
            np.put_along_axis(block[r], o[:, :B], F + 2 * t, axis=1)
            e = np.full((8, K), -1)
            for g in range(8):
                n = np.bincount(block[r, g], minlength=F + 2 * R)
                n[gone[r, g]] = C + 1
                b = np.argmin(n[:F + 2 * t])
                gone[r, g, b] = True
                s = o[g][block[r, g, o[g]] == b]
                e[g, :len(s)] = s
                block[r, g, s] = F + 2 * t + 1
            stay.append(e)
            kept.append(gcols(decode(q).astype(BF), e))
            sent.append(mx_ref.quantize(kept[r]))
        for r in range(N):
            p = (r - 1) % N
            h = layer(lay[r], sent[p])
            e = np.tile(np.arange(C), (8, 1))
            np.put_along_axis(e, first[r], np.tile(C + np.arange(B), (8, 1)), axis=1)
            for g in range(8):
                k = np.flatnonzero(stay[r][g] >= 0)
                e[g, stay[r][g, k]] = C + B + k + np.where(stay[p][g, k] >= 0, 0, K)
            now[r] = gcols(np.concatenate([now[r], made[r], h, kept[r]], axis=1), e)
    y, ob = np.zeros((N, 128, C), np.float32), np.zeros((N, 8, C), np.float32)
    oc, osc = np.zeros((N, 128, 4 * C), np.uint8), np.zeros((N, 16, C), np.uint8)
    for r in range(N):
        q = mx_ref.quantize(now[r])
        y[r] = mx_ref.matmul(mx_ref.quantize(v[r]), q)
        ob[r] = block[r]
        oc[r], osc[r] = emit(q)
    return {"y": y, "ob": ob, "oc": oc, "osc": osc}

@@ -1,0 +1,514 @@
+from concourse.mybir import dt, AluOpType as A, AxisListType, ActivationFunctionType as F
+
+C, B, R = 400, 80, 3
+NK = (4, 4, 3)
+NS = (64, 56, 48)
+BIG = 1e29
+FAR = 8192.0
+YO, HO, SO, END = 1608, 1928, 2184, 2440
+TW = (400, 336, 272, 208, 144, 128)
+SLOT = {"E": (0, 0)}
+for _c in range(24, 1, -1):
+    SLOT[_c] = ((25 - _c) // 4, (25 - _c) % 4)
+ON_S = (24, 23, 22, 21, 20, 19, 18, 5, 4, 3, 2)
+V_HI, V_LO = 17, 6
+HI = 16 * 18
+
+Q8, U8, BF, F16, F32, I32, U16 = "float8_e4m3fn_x4", "uint8", "bfloat16", "float16", "float32", "int32", "uint16"
+SCRATCH = {}
+
+
+def _sb(name, n, d):
+    SCRATCH[name] = ("sbuf", [128, n], d)
+
+
+for _k in range(8):
+    SCRATCH["p%d" % _k] = ("psum", [128, 512], F32)
+for _t in range(R):
+    _sb("st%d" % _t, END, BF)
+    _sb("qx%d" % _t, 402, Q8); _sb("sx%d" % _t, 402, U8)
+    _sb("qp%d" % _t, 192, Q8); _sb("sp%d" % _t, 192, U8)
+    _sb("qs%d" % _t, 128, Q8); _sb("ss%d" % _t, 128, U8)
+    _sb("qt%d" % _t, 192, Q8); _sb("sq%d" % _t, 192, U8)
+for _k in range(6):
+    _sb("tl%d" % _k, 4 * TW[_k], BF)
+for _n, _w, _d in (
+        ("st3", 1600, BF), ("qx3", 400, Q8), ("sx3", 400, U8), ("qc", 1488, Q8), ("sc", 1488, U8),
+        ("ub", 512, BF), ("vb", 512, BF), ("qu0", 128, Q8), ("su0", 128, U8), ("qu", 128, Q8), ("su", 128, U8),
+        ("qv", 128, Q8), ("sv", 128, U8), ("qw", 512, Q8), ("sw", 512, U8),
+        ("qe", 1024, Q8), ("se", 1024, U8), ("qo", 128, Q8), ("so", 128, U8),
+        ("ze", 520, BF), ("zo", 520, BF), ("zb", 512, BF), ("zero", 520, BF), ("tt", 512, BF),
+        ("pi", 24, I32), ("cf", 32, F32), ("uo", 8, U16), ("cs", 24, BF), ("cl", 24, BF),
+        ("dif", 128, BF), ("dg", 512, BF), ("d2", 32, F32), ("idn", 128, BF), ("m16", 400, BF), ("m4", 400, BF),
+        ("hold", 400, BF), ("pois", 400, BF), ("pick16", 400, BF), ("keep16", 400, BF), ("pick4", 400, BF), ("keep4", 400, BF),
+        ("cross", 32, F32), ("kc", 32, F32), ("k0", 32, F32), ("pg0", 100, F32), ("pg4", 100, F32), ("kk", 8, F32),
+        ("rowp", 400, F32), ("scn", 400, F32), ("sg0", 384, BF), ("sg1", 384, BF), ("sg2", 384, BF), ("tiny", 32, BF),
+        ("rs", 32, F32), ("rh", 12 * 144, BF), ("er", 400, BF), ("rr", 128, F32), ("mm", 400, F16), ("dd", 400, F16),
+        ("rk", 26, U16), ("pay", 400, F32), ("srt", 464, F32), ("sn", 400, F32),
+        ("lt", 80, BF), ("base", 32, F32), ("lab", 320, BF), ("col", 16, F32), ("kr", 32, F32), ("kt", 32, F32),
+        ("ea", 320, BF), ("eb", 322, BF), ("ec", 320, BF), ("zw", 400, BF), ("le", 640, BF), ("pb", 640, F32),
+        ("pos", 8, U16), ("sv1", 128, F32), ("sv2", 128, F32), ("po", 8, U16),
+        ("w80", 320, F32), ("to", 20, U16),
+        ("zm", 400, BF), ("zs", 400, BF), ("cc", 600, F32), ("eo", 100, U16),
+        ("yb", 400, F32), ("lf", 400, F32)):
+    _sb(_n, _w, _d)
+
+SEMAPHORES = ["cv", "ca", "ct", "cg", "ldx", "ldy", "ldu", "ldw", "ldz", "out", "loc",
+              "cnt0", "cnt1", "cnt2", "arr0", "arr1", "arr2"]
+
+LANE, GRP, PAR1, LQ, TQ, PAR0, LLAB, T1348, LPOS4, LPOS3, LHALF, GE5, GE7, GE9 = range(14)
+ISB, KADD, KTMP, TH0, TH1 = 14, 16, 18, 19, 20
+S0, VMIN, VV, V512, DCOL, KEY, K1, K2, K3, GG, S1, K4 = range(12)
+LAB0 = 129
+
+
+def rank_program(g, core, T, topo):
+    rank = T.rank_of(core)
+    if rank is None:
+        return
+    n_ranks = len(T.cores)
+    nxt, prv = T.cores[(rank + 1) % n_ranks], T.cores[(rank - 1) % n_ranks]
+    rid, pid = topo.addr(nxt, core)
+    mask_out = topo.mask(core, nxt)
+    n_out, n_in = len(topo.engines(core, nxt)), len(topo.engines(prv, core))
+
+    eng = {"v": g.vector, "a": g.scalar, "t": g.tensor, "g": g, "s": g.sync}
+    own = {"v": "cv", "a": "ca", "t": "ct", "g": "cg"}
+    count, seen, wrote, read = {}, {e: {} for e in eng}, {}, {}
+
+    def wait(e, tok):
+        sem, val, clock, _ = tok
+        if seen[e].get(sem, 0) < val:
+            eng[e].wait_ge(T.sem[sem], val)
+            seen[e][sem] = val
+        for s, v in clock.items():
+            if seen[e].get(s, 0) < v:
+                seen[e][s] = v
+
+    def order(e, rd, wr, acc):
+        need = []
+        for k in rd:
+            if k in wrote:
+                need.append(wrote[k])
+            if k[0] == "p" and k[1:].isdigit():
+                need += [x for x in read.get(k, []) if x[3] != e]
+        for k in wr:
+            if k in wrote and not (acc and wrote[k][3] == e):
+                need.append(wrote[k])
+            need += read.get(k, [])
+        for tok in sorted(need, key=lambda x: -x[1]):
+            wait(e, tok)
+
+    def note(tok, rd, wr):
+        for k in rd:
+            read.setdefault(k, []).append(tok)
+        for k in wr:
+            wrote[k] = tok
+            read[k] = []
+
+    def op(e, call, rd, wr, acc=False, sem=None, inc=1):
+        order(e, rd, wr, acc)
+        sem = sem or own[e]
+        call().then_inc(T.sem[sem], inc)
+        count[sem] = count.get(sem, 0) + inc
+        tok = (sem, count[sem], dict(seen[e]), e)
+        note(tok, rd, wr)
+        return tok
+
+    def dma(e, out, in_, rd, wr, sem):
+        return op(e, lambda: eng[e].dma_start(out, in_), rd, wr, sem=sem, inc=16)
+
+    def ts(out, in0, s1, s2, o0, o1, rd, wr):
+        if s2 is None:
+            return op("v", lambda: g.vector.tensor_scalar(out, in0, s1, None, o0), rd, wr)
+        return op("v", lambda: g.vector.tensor_scalar(out, in0, s1, s2, o0, o1), rd, wr)
+
+    def tt(out, in0, in1, o, rd, wr):
+        return op("v", lambda: g.vector.tensor_tensor(out, in0, in1, o), rd, wr)
+
+    def cp(out, in_, rd, wr):
+        return op("v", lambda: g.vector.tensor_copy(out, in_), rd, wr)
+
+    def ms(ap, val, wr):
+        return op("v", lambda: g.vector.memset(ap, val), [], wr)
+
+    def scan(out, d0, d1, init, o0, o1, rd, wr):
+        return op("v", lambda: g.vector.tensor_tensor_scan(out, d0, d1, init, o0, o1), rd, wr)
+
+    def red(out, in_, o, rd, wr):
+        return op("v", lambda: g.vector.tensor_reduce(out, in_, AxisListType.X, o), rd, wr)
+
+    def quant(q, s, in_, rd, wr):
+        return op("v", lambda: g.vector.quantize_mx(q, s, in_), rd, wr)
+
+    def act(out, in_, f, rd, wr, **kw):
+        return op("a", lambda: g.scalar.activation(out, in_, f, **kw), rd, wr)
+
+    def mx(bank, n, wq, ws, xq, xs, rd, start=True, stop=True):
+        return op("t", lambda: g.tensor.matmul_mx(T["p%d" % bank][:, 0:n], wq, ws, xq, xs, start, stop), rd, ["p%d" % bank], acc=not start)
+
+    def iota(out, pat, base, cm, wr, whole=False):
+        if whole:
+            return op("g", lambda: g.iota(out, pat, base, cm), [], wr)
+        return op("g", lambda: g.iota(out, pat, base, cm, allow_small_or_imprecise_dtypes=True), [], wr)
+
+    def send(out, in_, sem, rd):
+        order("g", rd, [], False)
+        g.remote_dma(out, in_, T.sem[sem], T.sem.loc, pid, rid, mask_out)
+        count["loc"] = count.get("loc", 0) + n_out
+
+    def cf(k):
+        return T.cf[:, k:k + 1]
+
+    def col(k):
+        return T.col[:, k:k + 1]
+
+    cc = [T.cc[:, 100 * k:100 * k + 100] for k in range(6)]
+    a80, g80, h80, i80 = [T.w80[:, B * k:B * k + B] for k in range(4)]
+    q1, q2, r2 = [T.rr[:, 32 * k:32 * k + 25] for k in range(3)]
+    hs_keys = [["%s%d_%d" % (n, t, b) for n in "HS" for b in range(4)] for t in range(R)]
+
+    ms(T.zero[:], 0.0, ["zero"])
+    dma("a", T.ub[:], T.u[:], [], ["ub"], "ldu")
+    dma("s", T.st0[:, 0:800], T.x[:, 0:800], [], ["xa"], "ldx")
+    dma("a", T.st0[:, 800:1600], T.x[:, 800:1600], [], ["xb"], "ldy")
+    dma("s", T.qw[:].bitcast(dt.uint8), T.wc[:], ["xa", "xb"], ["qw"], "ldw")
+    dma("s", T.sw[:], T.ws[:], [], ["sw"], "ldw")
+    wrote["qw"] = wrote["sw"] = dma("s", T.vb[:], T.v[:], [], ["vb"], "ldw")
+    for t in range(R):
+        dma("s", T["st%d" % t][:, HO:END], T.zero[:, 0:512], ["zero"], [], "ldz")
+    dma("s", T.tt[:, 4 * B:512], T.zero[:, 0:512 - 4 * B], ["zero"], ["ttz"] + sum(hs_keys, []), "ldz")
+
+    iota(T.pi[:, 0:1], [[0, 1]], 0, 1, ["pi"], True)
+    iota(T.pi[:, 16:24], [[16, 8]], 0, 0, ["ui"], True)
+    iota(T.m16[:], [[0, 25], [1, 16]], 0, 0, ["m16"])
+    iota(T.dif[:], [[1, 128]], 0, -1, ["dif"])
+    iota(T.dg[:], [[1, 8], [0, 64]], 0, 0, ["dg"])
+    iota(T.k0[:, 0:25], [[16, 25]], 0, 0, ["k0"])
+    iota(T.d2[:], [[1, 2], [0, 16]], 0, 0, ["d2"])
+    iota(T.pg0[:], [[16, 100]], 0, 0, ["pg0"])
+    iota(T.pay[:], [[512 + B, 5], [1, B]], 0, 0, ["pay"])
+    iota(T.zw[:, 0:B], [[1, B]], 65, 0, ["zw0"])
+    iota(T.m4[:], [[0, 100], [1, 4]], 0, 0, ["m4"])
+
+    def zeros(ap, n, wr):
+        act(ap, T.zero[:, 0:n], F.Copy, ["zero"], wr)
+
+    def plus(out, in_, b, rd, wr, scale=1.0):
+        act(out, in_, F.Identity, rd, wr, bias=b, scale=scale)
+
+    def unit(b, odd):
+        a = 256 * b + 128 * odd
+        quant(T.qe[:, a:a + 128], T.se[:, a:a + 128], (T.zo if odd else T.ze)[:, 3 - b:515 - b], ["zo" if odd else "ze"], ["qe%d" % (2 * b + odd)])
+
+    def blank(t):
+        quant(T["qp%d" % t][:, 64:192], T["sp%d" % t][:, 64:192], T.zero[:, 0:512], ["zero"], ["qp%d" % t, "sp%d" % t])
+
+    p0 = T.pi[:, 0:1]
+    ts(T.pi[:, 8:9], p0, 15, None, A.bitwise_and, None, ["pi"], ["pj0"])
+    ts(T.pi[:, 9:10], p0, 4, None, A.arith_shift_right, None, ["pi"], ["pj1"])
+    ts(T.pi[:, 10:11], p0, 4, 1, A.arith_shift_right, A.bitwise_and, ["pi"], ["pj2"])
+    ts(T.pi[:, 11:12], p0, 2, 3, A.arith_shift_right, A.bitwise_and, ["pi"], ["pj3"])
+    ts(T.pi[:, 12:13], p0, 3, None, A.bitwise_and, None, ["pi"], ["pj4"])
+    cp(T.uo[:], T.pi[:, 16:24], ["ui"], ["uo"])
+    cp(T.cf[:, 0:5], T.pi[:, 8:13], ["pj0", "pj1", "pj2", "pj3", "pj4"], ["lane"])
+    zeros(T.ze[:], 520, ["ze"])
+    zeros(T.zo[:], 520, ["zo"])
+    plus(cf(PAR0), cf(PAR1), 1.0, ["lane"], ["par0"], -1.0)
+    plus(cf(LLAB), cf(LANE), LAB0 / 8.0, ["lane"], ["llab"], 0.125)
+    for t in range(R):
+        zeros(T["st%d" % t][:, 1600:YO], 8, ["z%d" % t])
+    blank(0)
+    for k, n in ((GE5, 4.5), (GE7, 6.5), (GE9, 8.5)):
+        ts(cf(k), cf(LANE), n, FAR, A.is_gt, A.mult, ["lane"], ["ge%d" % k])
+    for t in range(R - 1):
+        ts(cf(ISB + t), cf(LANE), float(6 + 2 * t), 2.0, A.is_equal, A.mult, ["lane"], ["isb%d" % t])
+    ts(T.hold[:], T.m16[:], cf(LANE), -BIG, A.is_le, A.mult, ["m16", "lane"], ["hold"])
+    ts(T.pick16[:], T.m16[:], cf(LANE), None, A.is_equal, None, ["m16", "lane"], ["pick16"])
+    ts(T.idn[:], T.dif[:], 0.0, None, A.is_equal, None, ["dif"], ["idn"])
+    ts(T.pois[:], T.hold[:], -2.0, -BIG, A.mult, A.add, ["hold"], ["pois"])
+    ts(T.keep16[:], T.m16[:], 0.5, None, A.is_gt, None, ["m16"], ["keep16"])
+    ts(cf(KTMP), cf(GE5), cf(GE7), cf(GE9), A.add, A.add, ["ge%d" % GE5, "ge%d" % GE7, "ge%d" % GE9], ["ktmp"])
+    for t in range(R - 1):
+        ts(cf(KADD + t), cf(ISB + t), -float(144 + B), cf(GE5 + t), A.mult, A.subtract, ["isb%d" % t, "ge%d" % (GE5 + t)], ["kadd%d" % t])
+    act(T.ze[:, 3:515:4], T.idn[:], F.Identity, ["idn", "par0"], ["ze"], scale=cf(PAR0))
+    act(T.zo[:, 3:515:4], T.idn[:], F.Identity, ["idn", "lane"], ["zo"], scale=cf(PAR1))
+
+    def tile_zero(k):
+        lo = min(16 * c for c in range(2, 25) if SLOT[c][0] == k)
+        zeros(T["tl%d" % k][:, 4 * lo:4 * TW[k]], 4 * (TW[k] - lo), ["tl%d_%d" % (k, s) for s in range(4)])
+
+    for k in range(3):
+        tile_zero(k)
+    ts(col(KEY), cf(KTMP), cf(LLAB), 2.0 * (B + 144), A.add, A.add, ["ktmp", "llab"], ["key"])
+    ms(T.srt[:, C:464], FAR, ["srt1"])
+    ms(T.rs[:, V_LO:V_HI + 1], 128.0, ["rsv"])
+    quant(T.qu0[:], T.su0[:], T.ub[:], ["ub"], ["qu0"])
+    unit(0, 0)
+    cp(T.qu[:].bitcast(dt.uint32), T.qu0[:].bitcast(dt.uint32).indirect(T.uo[:]), ["qu0", "uo"], ["qu"])
+    act(T.su[:], T.su0[:].indirect(T.uo[:]), F.Copy, ["qu0", "uo"], ["su"])
+    for k in range(3, 6):
+        tile_zero(k)
+    unit(0, 1)
+    unit(1, 0)
+    unit(1, 1)
+    ts(T.zb[:], T.dg[:], cf(GRP), None, A.is_equal, None, ["dg", "lane"], ["zb"])
+    quant(T.qx0[:, 0:200], T.sx0[:, 0:200], T.st0[:, 0:800], ["xa"], ["qxa0"])
+    ts(T.cross[:], T.d2[:], cf(PAR1), FAR, A.not_equal, A.mult, ["d2", "lane"], ["cross"])
+    quant(T.qo[:], T.so[:], T.zb[:], ["zb"], ["qo"])
+    quant(T.qx0[:, 200:402], T.sx0[:, 200:402], T.st0[:, 800:YO], ["xb", "z0"], ["qxb0"])
+    plus(T.kc[:, 1:25], T.k0[:, 1:25], cf(LANE), ["k0", "lane"], ["kc"])
+    plus(T.kc[:, 0:1], cf(LANE), 16.0, ["lane"], ["kc0"])
+    plus(cf(LHALF), cf(LANE), 0.5, ["lane"], ["lhalf"])
+    plus(cf(TH0), cf(LANE), 0.5, ["lane"], ["th0"], -512.0)
+    plus(cf(TH1), cf(LANE), 0.5 - 512.0, ["lane"], ["th1"], -512.0)
+    plus(cf(LPOS4), cf(LANE), 240.0 + 48.0, ["lane"], ["lpos4"])
+    plus(cf(LPOS3), cf(LANE), 240.0 + 32.0, ["lane"], ["lpos3"])
+    plus(cf(T1348), cf(TQ), 1348.0, ["lane"], ["t1348"])
+    plus(T.kk[:, 0:4], T.k0[:, 0:4], cf(LHALF), ["k0", "lhalf"], ["kk"])
+    zeros(T.eb[:, 0:2], 2, ["eb0"])
+    plus(T.base[:], T.cross[:], col(KEY), ["cross", "key"], ["base"])
+    plus(T.pg4[:], T.pg0[:], cf(LANE), ["pg0", "lane"], ["pg4"])
+
+    def slot(c, n0, n1):
+        k, s = SLOT[c]
+        return T["tl%d" % k][:, 4 * n0 + s:4 * n1:4], "tl%d_%d" % (k, s)
+
+    def score(c):
+        return T.scn[:, 16 * c + 15:16 * c + 16], "scn_hi" if 16 * c >= HI else "scn_lo"
+
+    def rsum(c):
+        return T.rs[:, c:c + 1]
+
+    qoff = [sum(TW[:k]) for k in range(6)]
+
+    def tile_sum(k, start, stop):
+        a, b = qoff[k], qoff[k] + TW[k]
+        mx(2, TW[k], T.qo[:], T.so[:], T.qc[:, a:b], T.sc[:, a:b], ["qo", "qc%d" % k], start, stop)
+
+    def tile_quant(k):
+        a, b = qoff[k], qoff[k] + TW[k]
+        quant(T.qc[:, a:b], T.sc[:, a:b], T["tl%d" % k][:], ["tl%d_%d" % (k, s) for s in range(4)], ["qc%d" % k])
+
+    def layer(bank0, q, s, rd):
+        for b in range(4):
+            mx(bank0 + b, 128, T.qw[:, 128 * b:128 * b + 128], T.sw[:, 128 * b:128 * b + 128], q, s, ["qw"] + rd)
+
+    xkeys = ["xa", "xb"]
+
+    for t in range(R):
+        st, qx, sx = T["st%d" % t], T["qx%d" % t], T["sx%d" % t]
+        qxk = ["qxa%d" % t, "qxb%d" % t]
+        nk, ns, l1, l2 = NK[t], NS[t], 5 + 2 * t, 6 + 2 * t
+
+        mx(0, C, T.qu[:], T.su[:], qx[:, 0:C], sx[:, 0:C], ["qu", "su"] + qxk)
+        mx(1, C, T.qu[:], T.su[:], qx[:, 0:C], sx[:, 0:C], ["qu", "su"] + qxk)
+        if t == 0:
+            unit(2, 0)
+            unit(2, 1)
+        else:
+            blank(t)
+        tt(T.rowp[:, HI:C], T.p0[:, HI:C], T.pois[:, HI:C], A.min, ["p0", "pois"], ["rowp_hi"])
+        tt(T.rowp[:, 0:HI], T.p0[:, 0:HI], T.pois[:, 0:HI], A.min, ["p0", "pois"], ["rowp_lo"])
+        scan(T.scn[:, HI:C], T.hold[:, HI:C], T.rowp[:, HI:C], 0.0, A.add, A.max, ["hold", "rowp_hi"], ["scn_hi"])
+        scan(T.scn[:, 0:HI], T.hold[:, 0:HI], T.rowp[:, 0:HI], 0.0, A.add, A.max, ["hold", "rowp_lo"], ["scn_lo"])
+
+        def sign(i):
+            c = ON_S[i]
+            s, k = score(c)
+            act(T["sg%d" % (i % 3)][:, 0:16 * c], T.p1[:, 0:16 * c], F.Sign, ["p1", k], ["sg%d" % (i % 3)], bias=s, scale=-1.0)
+
+        def positive(i):
+            c = ON_S[i]
+            o, k = slot(c, 0, 16 * c)
+            act(o, T["sg%d" % (i % 3)][:, 0:16 * c], F.Relu, ["sg%d" % (i % 3)], [k, "rs%d" % c], accum_out=rsum(c))
+
+        sign(0)
+        for i in range(len(ON_S)):
+            if i + 1 < len(ON_S):
+                sign(i + 1)
+            positive(i)
+
+        def compare(c):
+            s, k = score(c)
+            o, ko = slot(c, 0, 16 * c)
+            ts(o, T.p0[:, 0:16 * c], s, None, A.is_lt, None, ["p0", k], [ko])
+
+        def along(c):
+            d0, k = slot(c, 0, 8 * c)
+            d1, k = slot(c, 8 * c, 16 * c)
+            e = 144 * (c - V_LO + 1)
+            scan(T.rh[:, e - 8 * c:e], d0, d1, -128.0, A.add, A.add, [k], ["rs%d" % c])
+
+        eo, ek = slot("E", 0, C)
+        ts(T.tiny[:, 0:16], T.p0[:, 16:32], score(0)[0], None, A.is_le, None, ["p0", "scn_lo"], ["tiny0"])
+        tt(eo, T.scn[:], T.p0[:, 0:C], A.is_ge, ["p0", "scn_lo", "scn_hi"], [ek])
+        ts(T.tiny[:, 16:32], T.p0[:, 0:16], score(1)[0], None, A.is_lt, None, ["p0", "scn_lo"], ["tiny1"])
+        compare(V_HI)
+        red(rsum(0), T.tiny[:, 0:16], A.add, ["tiny0"], ["rs0"])
+        red(rsum(1), T.tiny[:, 16:32], A.add, ["tiny1"], ["rs1"])
+        scan(T.er[:], T.keep16[:], eo, 0.0, A.mult, A.add, ["keep16", ek], ["er"])
+        for c in range(V_HI - 1, V_LO - 1, -1):
+            compare(c)
+            along(c + 1)
+            if c == 13:
+                tile_quant(2)
+            if c == 9:
+                tile_quant(0)
+                tile_sum(0, True, False)
+                tile_sum(2, False, False)
+                tile_quant(3)
+                tile_sum(3, False, False)
+        tt(q1, T.kc[:, 0:25], T.er[:, 15:C:16], A.subtract, ["kc", "kc0", "er"], ["q1"])
+        along(V_LO)
+        tile_quant(4)
+        tile_sum(4, False, False)
+        nv = V_HI - V_LO + 1
+        tt(T.rr[:, V_LO:V_HI + 1], T.rr[:, V_LO:V_HI + 1], T.rh[:, 143:144 * nv:144], A.subtract,
+           ["q1"] + ["rs%d" % c for c in range(V_LO, V_HI + 1)], ["q1"])
+        for k in (1, 5):
+            tile_quant(k)
+            tile_sum(k, False, k == 5)
+        tt(q2, q1, T.rs[:, 0:25], A.subtract, ["q1", "rsv"] + ["rs%d" % c for c in range(25)], ["q2"])
+        if t == 0:
+            unit(3, 0)
+        tt(T.mm[:], T.p2[:, 0:C], T.pick16[:], A.mult, ["p2", "pick16"], ["mm"])
+        scan(T.dd[:], T.keep16[:], T.mm[:], 0.0, A.mult, A.add, ["keep16", "mm"], ["dd"])
+        tt(r2, T.dd[:, 15:C:16], q2, A.add, ["dd", "q2"], ["r2"])
+        rk = T.rk[:, 0:25]
+        cp(rk, r2, ["r2"], ["rk"])
+
+        cp(T.srt[:, 0:C].indirect(rk), T.pay[:], ["rk", "pay"], ["srt"])
+        act(T.sg0[:, 0:B], T.srt[:, 0:B], F.Sign, ["srt", "th0"], ["sg0", "s0"], bias=cf(TH0), accum_out=col(S0))
+        act(T.sg1[:, 0:B], T.srt[:, 0:B], F.Sign, ["srt", "th1"], ["sg1", "s1"], bias=cf(TH1), accum_out=col(S1))
+        act(T.lab[:], T.srt[:, B:C], F.Identity, ["srt"], ["lab"], scale=1.0 / 4096, bias=(LAB0 - 0.39) / 8)
+        ts(T.lt[:], T.srt[:, 0:B], 1.0 / 512, LAB0 - 0.39, A.mult, A.add, ["srt"], ["lt"])
+        plus(a80, T.lt[:], 512.0 * LAB0, ["lt"], ["a80"], -512.0)
+        ts(T.kr[:], T.base[:], col(S0), col(S1), A.subtract, A.add, ["base", "s0", "s1"], ["kr"])
+        op("v", lambda: g.vector.transpose(T.kt[:], T.kr[:]), ["kr"], ["kt"])
+        red(col(VMIN), T.kt[:], A.min, ["kt"], ["vmin"])
+        cs, cl = T.cs[:, 8 * t:8 * t + 1], T.cl[:, 8 * t:8 * t + 1]
+        ts(cs, col(VMIN), 0.5, -8.31, A.mult, A.add, ["vmin"], ["cs%d" % t])
+        send(cl, cs, "cnt%d" % t, ["cs%d" % t])
+        ts(col(VV), cs, -2.0, col(VMIN), A.mult, A.add, ["cs%d" % t, "vmin"], ["vv"])
+
+        ts(T.ea[:], T.lab[:], col(VV), 145.0, A.is_equal, A.mult, ["lab", "vv"], ["ea"])
+        ts(T.eb[:, 2:322], T.lab[:], col(VV), 144.0, A.is_equal, A.mult, ["lab", "vv"], ["eb"])
+        plus(col(V512), col(VV), -512.0 * LAB0, ["vv"], ["v512"], 4096.0)
+        plus(col(DCOL), col(VV), 512.0 * (LAB0 + l2), ["vv"], ["dcol"], -4096.0)
+        scan(T.zw[:, B:C], T.ea[:], T.eb[:, 1:321], 0.0, A.add, A.subtract, ["ea", "eb", "eb0"], ["zw"])
+
+        on_v = range(nk - 2)
+        for k in (nk - 1, nk - 2):
+            lo, sg = B - 32 * (nk - 1 - k), "sg%d" % (k % 2)
+            act(T[sg][:, 0:C - lo], T.zw[:, lo:C], F.Sign, ["zw", "zw0", "kk"], ["pb%d" % k, sg],
+                bias=T.kk[:, k:k + 1], scale=-1.0, accum_out=T.pb[:, 160 * k + 159:160 * k + 160])
+        for k in on_v:
+            ts(T.le[:, 320 * k:320 * k + 320], T.zw[:, B:C], T.kk[:, k:k + 1], 2.0, A.is_lt, A.mult, ["zw", "kk"], ["le%d" % k])
+        for k in on_v:
+            scan(T.pb[:, 160 * k:160 * k + 160], T.le[:, 320 * k:320 * k + 160], T.le[:, 320 * k + 160:320 * k + 320],
+                 -320.0 - 32.0 * (nk - 1 - k), A.add, A.add, ["le%d" % k], ["pb%d" % k])
+        if nk == 3:
+            tt(g80, T.srt[:, 0:B], a80, A.add, ["srt", "a80"], ["g80"])
+        pbk = ["pb%d" % k for k in range(nk)]
+        lp = cf(LPOS4 if nk == 4 else LPOS3)
+        for h in range(2):
+            ts(T.pos[:, h:2 * nk:2], T.pb[:, 159:160 * nk:160], 0.5, lp, A.mult, A.add, pbk + ["lpos4", "lpos3"], ["pos%d" % h])
+        ts(T.sv1[:, 0:32 * nk], T.srt[:].indirect(T.pos[:, 0:2 * nk]), col(V512), float(C), A.subtract, A.min,
+           ["srt", "srt1", "pos0", "pos1", "v512"], ["sv1"])
+        op("v", lambda: g.vector.transpose(T.sv2[:, 0:32 * nk], T.sv1[:, 0:32 * nk]), ["sv1"], ["sv2"])
+        cp(T.po[:, 0:nk], T.sv2[:, 0:32 * nk:32], ["sv2"], ["po0"])
+        cp(T.po[:, nk:2 * nk], T.sv2[:, 16:32 * nk:32], ["sv2"], ["po1"])
+        po = T.po[:, 0:2 * nk]
+        qp, sp = T["qp%d" % t], T["sp%d" % t]
+        cp(qp[:, 0:32 * nk].bitcast(dt.uint32), qx[:].bitcast(dt.uint32).indirect(po), qxk + ["po0", "po1"], ["qp%d" % t])
+        act(sp[:, 0:32 * nk], sx[:].indirect(po), F.Copy, qxk + ["po0", "po1"], ["sp%d" % t])
+        if t == 0:
+            unit(3, 1)
+        w = 16 * nk
+        for b in range(4):
+            rd = ["qp%d" % t, "sp%d" % t, "qe%d" % (2 * b), "qe%d" % (2 * b + 1)]
+            e0, e1 = 256 * b, 256 * b + 128
+            mx(4 + b, 128, T.qe[:, e0:e0 + 128], T.se[:, e0:e0 + 128], qp[:, 0:128], sp[:, 0:128], rd, True, False)
+            mx(4 + b, 128, T.qe[:, e1:e1 + 128], T.se[:, e1:e1 + 128], qp[:, w:w + 128], sp[:, w:w + 128], rd, False, True)
+
+        if t == 0:
+            ts(T.pick4[:], T.m4[:], cf(LQ), None, A.is_equal, None, ["m4", "lane"], ["pick4"])
+        if nk == 4:
+            tt(g80, T.srt[:, 0:B], a80, A.add, ["srt", "a80"], ["g80"])
+        if t == 0:
+            ts(T.keep4[:], T.m4[:], 0.5, None, A.is_gt, None, ["m4"], ["keep4"])
+        tt(h80, g80, T.pick4[:, 0:B], A.mult, ["g80", "pick4"], ["h80"])
+        if t > 0:
+            ts(T.ec[:], T.lab[:], col(VV), col(DCOL), A.is_equal, A.mult, ["lab", "vv", "dcol"], ["ec"])
+
+        for b in range(4):
+            act(st[:, SO + b:SO + 4 * w:4], T["p%d" % (4 + b)][:, 0:w], F.Copy, ["p%d" % (4 + b)], ["S%d_%d" % (t, b)])
+        scan(i80, T.keep4[:, 0:B], h80, 0.0, A.mult, A.add, ["keep4", "h80"], ["i80"])
+        ts(T.to[:], T.w80[:, 3 * B + 3:4 * B:4], 4.0, cf(TQ), A.mult, A.add, ["i80", "lane"], ["to"])
+        qs, ss, qt, sq = T["qs%d" % t], T["ss%d" % t], T["qt%d" % t], T["sq%d" % t]
+        quant(qs[:], ss[:], st[:, HO:END], hs_keys[t], ["qs%d" % t])
+        send(qt[:, 128:128 + ns].bitcast(dt.uint8), qs[:, 64:64 + ns].bitcast(dt.uint8), "arr%d" % t, ["qs%d" % t])
+        send(sq[:, 128:128 + ns], ss[:, 64:64 + ns], "arr%d" % t, ["qs%d" % t])
+
+        act(T.tt[:, 0:4 * B], st[:, 0:1600].indirect(T.to[:]), F.Copy, xkeys + ["to"], ["tt"])
+        tt(T.zm[:], T.zw[:].indirect(rk), T.pick4[:], A.mult, ["zw", "zw0", "rk", "pick4"], ["zm"])
+        quant(qt[:, 0:128], sq[:, 0:128], T.tt[:], ["tt", "ttz"], ["qt%d" % t])
+        layer(0, qt[:, 0:128], sq[:, 0:128], ["qt%d" % t, "sw"])
+        scan(T.zs[:], T.keep4[:], T.zm[:], 0.0, A.mult, A.add, ["keep4", "zm"], ["zs"])
+        if t == 0:
+            ts(T.ec[:], T.lab[:], col(VV), col(DCOL), A.is_equal, A.mult, ["lab", "vv", "dcol"], ["ec"])
+        z = T.zs[:, 3:C:4]
+        plus(T.sn[:, 0:B], g80, 512.0 * l1, ["g80"], ["sn0"])
+        plus(cc[1], z, cf(T1348), ["zs", "t1348"], ["c2"], 4.0)
+        ts(cc[0], z, 64.5, -4096.0, A.is_lt, A.mult, ["zs"], ["c1"])
+        for b in range(4):
+            act(st[:, YO + b:HO:4], T["p%d" % b][:, 0:B], F.Copy, ["p%d" % b], ["Y%d_%d" % (t, b)], scale=0.03125)
+        wrote["cl%d" % t] = ("cnt%d" % t, n_in, {}, "r")
+        ts(cc[4], z, cl, 256.0, A.is_gt, A.mult, ["zs", "cl%d" % t], ["c5"])
+        tt(cc[2], cc[0], cc[1], A.add, ["c1", "c2"], ["c3"])
+        nx, u = T["st%d" % (t + 1)], t + 1
+        if u < R:
+            ts(col(GG), cf(LLAB), col(VV), FAR, A.is_equal, A.mult, ["llab", "vv"], ["gg"])
+        tt(cc[3], cc[2], T.pg4[:], A.max, ["c3", "pg4"], ["c4"])
+        tt(cc[5], cc[3], cc[4], A.add, ["c4", "c5"], ["c6"])
+        cp(T.eo[:], cc[5], ["c6"], ["eo"])
+        tt(T.sn[:, B:C], T.srt[:, B:C], T.ec[:], A.add, ["srt", "ec"], ["sn"])
+        if u == R:
+            quant(T.qv[:], T.sv[:], T.vb[:], ["vb"], ["qv"])
+            act(T.pay[:], T.sn[:].indirect(rk), F.Copy, ["sn", "sn0", "rk"], ["pay"])
+
+        wrote["land%d" % t] = ("arr%d" % t, 2 * n_in, {}, "r")
+        layer(4, qt[:, ns:128 + ns], sq[:, ns:128 + ns], ["qt%d" % t, "sw", "land%d" % t])
+        for b in range(4):
+            act(st[:, HO + b:HO + 4 * ns:4], T["p%d" % (4 + b)][:, 128 - ns:128], F.Copy, ["p%d" % (4 + b)], ["H%d_%d" % (t, b)], scale=0.03125)
+        every = xkeys + hs_keys[t] + ["z%d" % t, "eo"] + ["Y%d_%d" % (t, b) for b in range(4)]
+        xkeys = ["xa%d" % u, "xb%d" % u]
+        cp(nx[:, 0:800], st[:].indirect(T.eo[:, 0:50]), every, [xkeys[0]])
+        act(nx[:, 800:1600], st[:].indirect(T.eo[:, 50:100]), F.Copy, every, [xkeys[1]])
+        last = 402 if u < R else C
+        quant(T["qx%d" % u][:, 0:200], T["sx%d" % u][:, 0:200], nx[:, 0:800], [xkeys[0]], ["qxa%d" % u])
+        quant(T["qx%d" % u][:, 200:last], T["sx%d" % u][:, 200:last], nx[:, 800:4 * last], [xkeys[1], "z%d" % u], ["qxb%d" % u])
+        if u < R:
+            act(T.pay[:], T.sn[:].indirect(rk), F.Copy, ["sn", "sn0", "rk"], ["pay"])
+            act(col(K2), cs, F.Identity, ["cs%d" % t, "isb%d" % t, "kadd%d" % t], ["k2"], scale=cf(ISB + t), bias=cf(KADD + t))
+            plus(col(K1), col(S0), col(KEY), ["s0", "key"], ["k1"], -1.0)
+            plus(col(K3), col(GG), col(K2), ["gg", "k2"], ["k3"])
+            plus(col(K4), col(S1), col(K1), ["s1", "k1"], ["k4"])
+            plus(col(KEY), col(K4), col(K3), ["k4", "k3"], ["key"])
+            plus(T.base[:], T.cross[:], col(KEY), ["cross", "key"], ["base"])
+
+    dma("s", T.oc[:, 0:800], T.qx3[:, 0:200].bitcast(dt.uint8), ["qxa3"], [], "out")
+    mx(0, 200, T.qv[:], T.sv[:], T.qx3[:, 0:200], T.sx3[:, 0:200], ["qv", "qxa3"])
+    dma("s", T.oc[:, 800:1600], T.qx3[:, 200:C].bitcast(dt.uint8), ["qxb3"], [], "out")
+    mx(1, 200, T.qv[:], T.sv[:], T.qx3[:, 200:C], T.sx3[:, 200:C], ["qv", "qxb3"])
+    act(T.yb[:, 0:200], T.p0[:, 0:200], F.Copy, ["p0"], ["ya"])
+    cp(T.yb[:, 200:C], T.p1[:, 0:200], ["p1"], ["yb"])
+    dma("a", T.y[:], T.yb[:], ["ya", "yb"], [], "out")
+    ts(T.er[:], T.pay[:], 1.0 / 512, LAB0 - 0.39, A.mult, A.add, ["pay"], ["er"])
+    for k in range(4):
+        dma("s", T.osc[4 * k:4 * k + 4, :], T.sx3[32 * k:32 * k + 4, :], ["qxa3", "qxb3"], [], "out")
+    ts(T.lf[:], T.er[:], -float(LAB0), None, A.add, None, ["er"], ["lf"])
+    dma("a", T.ob[:], T.lf[0:128:16, :], ["lf"], [], "out")
+    for sem in ("cv", "ca", "ct", "cg", "ldx", "ldy", "ldu", "ldw", "ldz", "loc", "out"):
+        g.wait_ge(T.sem[sem], count[sem])

@@ -5,14 +5,19 @@ NK = (4, 4, 3)
 NS = (64, 56, 48)
 BIG = 1e29
 FAR = 8192.0
-YO, HO, SO, END = 1608, 1928, 2184, 2440
+SPARE = 4 * C
+HEAD = 128
+TAIL = 272
 TW = (400, 336, 272, 208, 144, 128)
 SLOT = {"E": (0, 0)}
 for _c in range(24, 1, -1):
     SLOT[_c] = ((25 - _c) // 4, (25 - _c) % 4)
-ON_S = (24, 23, 22, 21, 20, 19, 18, 5, 4, 3, 2)
-V_HI, V_LO = 17, 6
-HI = 16 * 18
+ON_S = (5, 4, 3, 2, 7, 6, 16, 15, 14, 13, 12, 11, 10, 9, 8)
+V_LO = 17
+V_PLAN = (24, 23, 22, "q0", 21, 20, "q5", 19, 18, "q1", 17, "er", "q2", -24, -23, -22, -21, "q3", -20, -19, -18, "q4", -17)
+STEP = 2048.0
+SLOT0 = 129
+FINE = 128.0 * STEP
 
 Q8, U8, BF, F16, F32, I32, U16 = "float8_e4m3fn_x4", "uint8", "bfloat16", "float16", "float32", "int32", "uint16"
 SCRATCH = {}
@@ -25,41 +30,37 @@ def _sb(name, n, d):
 for _k in range(8):
     SCRATCH["p%d" % _k] = ("psum", [128, 512], F32)
 for _t in range(R):
-    _sb("st%d" % _t, END, BF)
-    _sb("qx%d" % _t, 402, Q8); _sb("sx%d" % _t, 402, U8)
-    _sb("qp%d" % _t, 192, Q8); _sb("sp%d" % _t, 192, U8)
     _sb("qs%d" % _t, 128, Q8); _sb("ss%d" % _t, 128, U8)
     _sb("qt%d" % _t, 192, Q8); _sb("sq%d" % _t, 192, U8)
+    _sb("cs%d" % _t, 4, F32); _sb("cl%d" % _t, 4, F32)
 for _k in range(6):
     _sb("tl%d" % _k, 4 * TW[_k], BF)
 for _n, _w, _d in (
-        ("st3", 1600, BF), ("qx3", 400, Q8), ("sx3", 400, U8), ("qc", 1488, Q8), ("sc", 1488, U8),
+        ("st", SPARE + 256, BF), ("dx", SPARE + 8, BF), ("qx", C, Q8), ("sx", C, U8), ("qc", 1488, Q8), ("sc", 1488, U8),
         ("ub", 512, BF), ("vb", 512, BF), ("qu0", 128, Q8), ("su0", 128, U8), ("qu", 128, Q8), ("su", 128, U8),
         ("qv", 128, Q8), ("sv", 128, U8), ("qw", 512, Q8), ("sw", 512, U8),
-        ("qe", 1024, Q8), ("se", 1024, U8), ("qo", 128, Q8), ("so", 128, U8),
-        ("ze", 520, BF), ("zo", 520, BF), ("zb", 512, BF), ("zero", 520, BF), ("tt", 512, BF),
-        ("pi", 24, I32), ("cf", 32, F32), ("uo", 8, U16), ("cs", 24, BF), ("cl", 24, BF),
-        ("dif", 128, BF), ("dg", 512, BF), ("d2", 32, F32), ("idn", 128, BF), ("m16", 400, BF), ("m4", 400, BF),
-        ("hold", 400, BF), ("pois", 400, BF), ("pick16", 400, BF), ("keep16", 400, BF), ("pick4", 400, BF), ("keep4", 400, BF),
-        ("cross", 32, F32), ("kc", 32, F32), ("k0", 32, F32), ("pg0", 100, F32), ("pg4", 100, F32), ("kk", 8, F32),
-        ("rowp", 400, F32), ("scn", 400, F32), ("sg0", 384, BF), ("sg1", 384, BF), ("sg2", 384, BF), ("tiny", 32, BF),
-        ("rs", 32, F32), ("rh", 12 * 144, BF), ("er", 400, BF), ("rr", 128, F32), ("mm", 400, F16), ("dd", 400, F16),
-        ("rk", 26, U16), ("pay", 400, F32), ("srt", 464, F32), ("sn", 400, F32),
-        ("lt", 80, BF), ("base", 32, F32), ("lab", 320, BF), ("col", 16, F32), ("kr", 32, F32), ("kt", 32, F32),
-        ("ea", 320, BF), ("eb", 322, BF), ("ec", 320, BF), ("zw", 400, BF), ("le", 640, BF), ("pb", 640, F32),
-        ("pos", 8, U16), ("sv1", 128, F32), ("sv2", 128, F32), ("po", 8, U16),
-        ("w80", 320, F32), ("to", 20, U16),
-        ("zm", 400, BF), ("zs", 400, BF), ("cc", 600, F32), ("eo", 100, U16),
-        ("yb", 400, F32), ("lf", 400, F32)):
+        ("qe", 512, Q8), ("se", 512, U8), ("qo", 128, Q8), ("so", 128, U8),
+        ("ze", 520, BF), ("zb", 512, BF), ("tt", 512, BF), ("sb", 512, BF), ("yt", 320, BF), ("zt", 256, BF),
+        ("pi", 24, I32), ("cf", 32, F32), ("uo", 8, U16),
+        ("dif", 128, BF), ("dg", 512, BF), ("d2", 32, F32), ("m16", C, BF), ("m4", B, BF), ("ab", C, BF),
+        ("hold", C, BF), ("pois", C, BF), ("pick16", C, BF), ("keep16", C, BF), ("kq", C, F16), ("pick4", B, BF), ("keep4", B, BF),
+        ("cross", 32, F32), ("k0", 32, F32), ("kk", 4, F32), ("kc2", 16, F32), ("own", 16, F32), ("dum", 16, F32), ("pay0", C, F32),
+        ("rowp", C, F32), ("scn", C, F32), ("sg0", 384, BF), ("sg1", 384, BF), ("sg2", 384, BF),
+        ("rs", 32, F32), ("rh", 192 * (25 - V_LO), BF), ("er", C, F16), ("rr", 96, F32), ("mm", C, F16), ("dd", C, F16),
+        ("rk", 26, U16), ("pay", C, F32), ("srt", C + 8, F32),
+        ("lt", B, BF), ("base", 64, F32), ("lab", 320, BF), ("col", 16, F32), ("kr", 64, F32), ("kt", 64, F32),
+        ("ind", 320, BF), ("cnt", 320, BF), ("le", 320, BF), ("pb", 640, F32),
+        ("pos", 4, U16), ("xg", 64, F32), ("xs", 64, F32), ("gl", 16, U16), ("off", 16, F32), ("slf", 16, F32), ("sl", 16, U16),
+        ("hm", 48, F32), ("hl", 16, U16), ("w80", 240, F32), ("to", 20, U16),
+        ("lc", 64, F32), ("lu", 26, U16), ("tb", 64, F32), ("yb", C, F32), ("lf", C, F32)):
     _sb(_n, _w, _d)
 
-SEMAPHORES = ["cv", "ca", "ct", "cg", "ldx", "ldy", "ldu", "ldw", "ldz", "out", "loc",
-              "cnt0", "cnt1", "cnt2", "arr0", "arr1", "arr2"]
+SEMAPHORES = (["cv", "ca", "ct", "cg", "ldu", "ldx", "ldy", "ldw", "lds", "ldv", "out", "loc"]
+              + ["cnt%d" % _t for _t in range(R)] + ["arr%d" % _t for _t in range(R)])
 
-LANE, GRP, PAR1, LQ, TQ, PAR0, LLAB, T1348, LPOS4, LPOS3, LHALF, GE5, GE7, GE9 = range(14)
-ISB, KADD, KTMP, TH0, TH1 = 14, 16, 18, 19, 20
-S0, VMIN, VV, V512, DCOL, KEY, K1, K2, K3, GG, S1, K4 = range(12)
-LAB0 = 129
+LANE, GRP, PAR, LQ, TQ, LABL, TH0, TH1, LHALF, KC, LG0, PFAR, PAR16 = range(13)
+FARS, LNEW = 16, 20
+S0, S1, VM1, VM2, VV, CNT, ISV, LG, LGF, KEY2, KEY1 = range(11)
 
 
 def rank_program(g, core, T, topo):
@@ -72,443 +73,463 @@ def rank_program(g, core, T, topo):
     mask_out = topo.mask(core, nxt)
     n_out, n_in = len(topo.engines(core, nxt)), len(topo.engines(prv, core))
 
+    def v(name, lo=0, hi=None, step=1):
+        hi = SCRATCH[name][1][1] if hi is None else hi
+        ap = T[name][:, lo:hi] if step == 1 else T[name][:, lo:hi:step]
+        return ap, [(name, range(0, 1) if SCRATCH[name][0] == "psum" else range(lo, hi, step))]
+
+    def words(x):
+        return x[0].bitcast(dt.uint32), x[1]
+
+    def raw(x):
+        return x[0].bitcast(dt.uint8), x[1]
+
+    def by(x, off):
+        return x[0].indirect(off[0]), x[1], off[1]
+
+    def ap(x):
+        return x[0] if isinstance(x, tuple) else x
+
     eng = {"v": g.vector, "a": g.scalar, "t": g.tensor, "g": g, "s": g.sync}
     own = {"v": "cv", "a": "ca", "t": "ct", "g": "cg"}
-    count, seen, wrote, read = {}, {e: {} for e in eng}, {}, {}
+    count, seen = {}, {e: {} for e in eng}
+    wrote = {n: {} for n in SCRATCH}
+    read = {n: {} for n in SCRATCH}
 
     def wait(e, tok):
         sem, val, clock, _ = tok
         if seen[e].get(sem, 0) < val:
             eng[e].wait_ge(T.sem[sem], val)
             seen[e][sem] = val
-        for s, v in clock.items():
-            if seen[e].get(s, 0) < v:
-                seen[e][s] = v
+        for s, n in clock.items():
+            if seen[e].get(s, 0) < n:
+                seen[e][s] = n
 
     def order(e, rd, wr, acc):
-        need = []
-        for k in rd:
-            if k in wrote:
-                need.append(wrote[k])
-            if k[0] == "p" and k[1:].isdigit():
-                need += [x for x in read.get(k, []) if x[3] != e]
-        for k in wr:
-            if k in wrote and not (acc and wrote[k][3] == e):
-                need.append(wrote[k])
-            need += read.get(k, [])
-        for tok in sorted(need, key=lambda x: -x[1]):
+        need = {}
+
+        def add(tok):
+            if tok[1] > need.get(tok[0], (0, 0))[1]:
+                need[tok[0]] = tok
+
+        for name, cols in rd:
+            for c in cols:
+                if c in wrote[name]:
+                    add(wrote[name][c])
+            if SCRATCH[name][0] == "psum":
+                for x in read[name].get(0, {}).values():
+                    if x[3] != e:
+                        add(x)
+        for name, cols in wr:
+            for c in cols:
+                if c in wrote[name] and not (acc and wrote[name][c][3] == e):
+                    add(wrote[name][c])
+                for x in read[name].get(c, {}).values():
+                    add(x)
+        for tok in sorted(need.values(), key=lambda x: -len(x[2])):
             wait(e, tok)
 
     def note(tok, rd, wr):
-        for k in rd:
-            read.setdefault(k, []).append(tok)
-        for k in wr:
-            wrote[k] = tok
-            read[k] = []
+        for name, cols in rd:
+            for c in cols:
+                read[name].setdefault(c, {})[tok[0]] = tok
+        for name, cols in wr:
+            for c in cols:
+                wrote[name][c] = tok
+                read[name][c] = {}
 
-    def op(e, call, rd, wr, acc=False, sem=None, inc=1):
+    def op(e, call, ins, outs, acc=False, sem=None, inc=1):
+        rd = [r for x in ins if isinstance(x, tuple) for part in x[1:] for r in part] + [r for x in outs for part in x[2:] for r in part]
+        wr = [r for x in outs for r in x[1]]
         order(e, rd, wr, acc)
         sem = sem or own[e]
         call().then_inc(T.sem[sem], inc)
         count[sem] = count.get(sem, 0) + inc
-        tok = (sem, count[sem], dict(seen[e]), e)
-        note(tok, rd, wr)
-        return tok
+        note((sem, count[sem], dict(seen[e]), e), rd, wr)
 
-    def dma(e, out, in_, rd, wr, sem):
-        return op(e, lambda: eng[e].dma_start(out, in_), rd, wr, sem=sem, inc=16)
+    def load(e, out, src, sem, after=()):
+        op(e, lambda: eng[e].dma_start(out[0], src), list(after), [out], sem=sem, inc=16)
 
-    def ts(out, in0, s1, s2, o0, o1, rd, wr):
+    def store(e, dst, in_):
+        op(e, lambda: eng[e].dma_start(dst, in_[0]), [in_], [], sem="out", inc=16)
+
+    def ts(out, in0, s1, s2, o0, o1=None):
         if s2 is None:
-            return op("v", lambda: g.vector.tensor_scalar(out, in0, s1, None, o0), rd, wr)
-        return op("v", lambda: g.vector.tensor_scalar(out, in0, s1, s2, o0, o1), rd, wr)
+            return op("v", lambda: g.vector.tensor_scalar(out[0], in0[0], ap(s1), None, o0), [in0, s1], [out])
+        return op("v", lambda: g.vector.tensor_scalar(out[0], in0[0], ap(s1), ap(s2), o0, o1), [in0, s1, s2], [out])
 
-    def tt(out, in0, in1, o, rd, wr):
-        return op("v", lambda: g.vector.tensor_tensor(out, in0, in1, o), rd, wr)
+    def tt(out, in0, in1, o):
+        op("v", lambda: g.vector.tensor_tensor(out[0], in0[0], in1[0], o), [in0, in1], [out])
 
-    def cp(out, in_, rd, wr):
-        return op("v", lambda: g.vector.tensor_copy(out, in_), rd, wr)
+    def cp(out, in_):
+        op("v", lambda: g.vector.tensor_copy(out[0], in_[0]), [in_], [out])
 
-    def ms(ap, val, wr):
-        return op("v", lambda: g.vector.memset(ap, val), [], wr)
+    def ms(out, val):
+        op("v", lambda: g.vector.memset(out[0], val), [], [out])
 
-    def scan(out, d0, d1, init, o0, o1, rd, wr):
-        return op("v", lambda: g.vector.tensor_tensor_scan(out, d0, d1, init, o0, o1), rd, wr)
+    def scan(out, d0, d1, init, o0, o1):
+        op("v", lambda: g.vector.tensor_tensor_scan(out[0], d0[0], d1[0], init, o0, o1), [d0, d1], [out])
 
-    def red(out, in_, o, rd, wr):
-        return op("v", lambda: g.vector.tensor_reduce(out, in_, AxisListType.X, o), rd, wr)
+    def red(out, in_, o):
+        op("v", lambda: g.vector.tensor_reduce(out[0], in_[0], AxisListType.X, o), [in_], [out])
 
-    def quant(q, s, in_, rd, wr):
-        return op("v", lambda: g.vector.quantize_mx(q, s, in_), rd, wr)
+    def turn(out, in_):
+        op("v", lambda: g.vector.transpose(out[0], in_[0]), [in_], [out])
 
-    def act(out, in_, f, rd, wr, **kw):
-        return op("a", lambda: g.scalar.activation(out, in_, f, **kw), rd, wr)
+    def quant(q, s, lo, hi, in_):
+        qq, ss = v(q, lo, hi), v(s, lo, hi)
+        op("v", lambda: g.vector.quantize_mx(qq[0], ss[0], in_[0]), [in_], [qq, ss])
 
-    def mx(bank, n, wq, ws, xq, xs, rd, start=True, stop=True):
-        return op("t", lambda: g.tensor.matmul_mx(T["p%d" % bank][:, 0:n], wq, ws, xq, xs, start, stop), rd, ["p%d" % bank], acc=not start)
+    def act(out, in_, f, bias=None, scale=None, total=None):
+        kw = {k: ap(x) for k, x in (("bias", bias), ("scale", scale), ("accum_out", total)) if x is not None}
+        op("a", lambda: g.scalar.activation(out[0], in_[0], f, **kw), [in_, bias, scale], [out] + ([total] if total else []))
 
-    def iota(out, pat, base, cm, wr, whole=False):
+    def plus(out, in_, b, scale=1.0):
+        act(out, in_, F.Identity, bias=b, scale=scale)
+
+    def mx(bank, w, x, start=True, stop=True):
+        a = [v(w[0], w[2], w[3]), v(w[1], w[2], w[3]), v(x[0], x[2], x[3]), v(x[1], x[2], x[3])]
+        out = v("p%d" % bank, 0, x[3] - x[2])
+        op("t", lambda: g.tensor.matmul_mx(out[0], a[0][0], a[1][0], a[2][0], a[3][0], start, stop), a, [out], acc=not start)
+
+    def iota(out, pat, base, cm, whole=False):
         if whole:
-            return op("g", lambda: g.iota(out, pat, base, cm), [], wr)
-        return op("g", lambda: g.iota(out, pat, base, cm, allow_small_or_imprecise_dtypes=True), [], wr)
+            return op("g", lambda: g.iota(out[0], pat, base, cm), [], [out])
+        return op("g", lambda: g.iota(out[0], pat, base, cm, allow_small_or_imprecise_dtypes=True), [], [out])
 
-    def send(out, in_, sem, rd):
-        order("g", rd, [], False)
-        g.remote_dma(out, in_, T.sem[sem], T.sem.loc, pid, rid, mask_out)
+    def fill(out, val=0):
+        iota(out, [[0, len(out[1][0][1])]], val, 0)
+
+    def send(out, in_, sem):
+        order("g", in_[1], [], False)
+        g.remote_dma(out[0], in_[0], T.sem[sem], T.sem.loc, pid, rid, mask_out)
         count["loc"] = count.get("loc", 0) + n_out
 
+    def landed(views, sem, n):
+        note((sem, n, {}, "r"), [], [r for x in views for r in x[1]])
+
     def cf(k):
-        return T.cf[:, k:k + 1]
+        return v("cf", k, k + 1)
 
     def col(k):
-        return T.col[:, k:k + 1]
+        return v("col", k, k + 1)
 
-    cc = [T.cc[:, 100 * k:100 * k + 100] for k in range(6)]
-    a80, g80, h80, i80 = [T.w80[:, B * k:B * k + B] for k in range(4)]
-    q1, q2, r2 = [T.rr[:, 32 * k:32 * k + 25] for k in range(3)]
-    hs_keys = [["%s%d_%d" % (n, t, b) for n in "HS" for b in range(4)] for t in range(R)]
+    def pi(k):
+        return v("pi", k, k + 1)
 
-    ms(T.zero[:], 0.0, ["zero"])
-    dma("a", T.ub[:], T.u[:], [], ["ub"], "ldu")
-    dma("s", T.st0[:, 0:800], T.x[:, 0:800], [], ["xa"], "ldx")
-    dma("a", T.st0[:, 800:1600], T.x[:, 800:1600], [], ["xb"], "ldy")
-    dma("s", T.qw[:].bitcast(dt.uint8), T.wc[:], ["xa", "xb"], ["qw"], "ldw")
-    dma("s", T.sw[:], T.ws[:], [], ["sw"], "ldw")
-    wrote["qw"] = wrote["sw"] = dma("s", T.vb[:], T.v[:], [], ["vb"], "ldw")
-    for t in range(R):
-        dma("s", T["st%d" % t][:, HO:END], T.zero[:, 0:512], ["zero"], [], "ldz")
-    dma("s", T.tt[:, 4 * B:512], T.zero[:, 0:512 - 4 * B], ["zero"], ["ttz"] + sum(hs_keys, []), "ldz")
+    def pages(lo, hi):
+        return v("st", 4 * lo, 4 * hi)
 
-    iota(T.pi[:, 0:1], [[0, 1]], 0, 1, ["pi"], True)
-    iota(T.pi[:, 16:24], [[16, 8]], 0, 0, ["ui"], True)
-    iota(T.m16[:], [[0, 25], [1, 16]], 0, 0, ["m16"])
-    iota(T.dif[:], [[1, 128]], 0, -1, ["dif"])
-    iota(T.dg[:], [[1, 8], [0, 64]], 0, 0, ["dg"])
-    iota(T.k0[:, 0:25], [[16, 25]], 0, 0, ["k0"])
-    iota(T.d2[:], [[1, 2], [0, 16]], 0, 0, ["d2"])
-    iota(T.pg0[:], [[16, 100]], 0, 0, ["pg0"])
-    iota(T.pay[:], [[512 + B, 5], [1, B]], 0, 0, ["pay"])
-    iota(T.zw[:, 0:B], [[1, B]], 65, 0, ["zw0"])
-    iota(T.m4[:], [[0, 100], [1, 4]], 0, 0, ["m4"])
+    def quant_x(lo, hi):
+        quant("qx", "sx", lo, hi, pages(lo, hi))
 
-    def zeros(ap, n, wr):
-        act(ap, T.zero[:, 0:n], F.Copy, ["zero"], wr)
+    QU, QV, QO = ("qu", "su", 0, 128), ("qv", "sv", 0, 128), ("qo", "so", 0, 128)
+    g80, h80, i80 = [v("w80", B * k, B * k + B) for k in range(3)]
 
-    def plus(out, in_, b, rd, wr, scale=1.0):
-        act(out, in_, F.Identity, rd, wr, bias=b, scale=scale)
-
-    def unit(b, odd):
-        a = 256 * b + 128 * odd
-        quant(T.qe[:, a:a + 128], T.se[:, a:a + 128], (T.zo if odd else T.ze)[:, 3 - b:515 - b], ["zo" if odd else "ze"], ["qe%d" % (2 * b + odd)])
-
-    def blank(t):
-        quant(T["qp%d" % t][:, 64:192], T["sp%d" % t][:, 64:192], T.zero[:, 0:512], ["zero"], ["qp%d" % t, "sp%d" % t])
-
-    p0 = T.pi[:, 0:1]
-    ts(T.pi[:, 8:9], p0, 15, None, A.bitwise_and, None, ["pi"], ["pj0"])
-    ts(T.pi[:, 9:10], p0, 4, None, A.arith_shift_right, None, ["pi"], ["pj1"])
-    ts(T.pi[:, 10:11], p0, 4, 1, A.arith_shift_right, A.bitwise_and, ["pi"], ["pj2"])
-    ts(T.pi[:, 11:12], p0, 2, 3, A.arith_shift_right, A.bitwise_and, ["pi"], ["pj3"])
-    ts(T.pi[:, 12:13], p0, 3, None, A.bitwise_and, None, ["pi"], ["pj4"])
-    cp(T.uo[:], T.pi[:, 16:24], ["ui"], ["uo"])
-    cp(T.cf[:, 0:5], T.pi[:, 8:13], ["pj0", "pj1", "pj2", "pj3", "pj4"], ["lane"])
-    zeros(T.ze[:], 520, ["ze"])
-    zeros(T.zo[:], 520, ["zo"])
-    plus(cf(PAR0), cf(PAR1), 1.0, ["lane"], ["par0"], -1.0)
-    plus(cf(LLAB), cf(LANE), LAB0 / 8.0, ["lane"], ["llab"], 0.125)
-    for t in range(R):
-        zeros(T["st%d" % t][:, 1600:YO], 8, ["z%d" % t])
-    blank(0)
-    for k, n in ((GE5, 4.5), (GE7, 6.5), (GE9, 8.5)):
-        ts(cf(k), cf(LANE), n, FAR, A.is_gt, A.mult, ["lane"], ["ge%d" % k])
-    for t in range(R - 1):
-        ts(cf(ISB + t), cf(LANE), float(6 + 2 * t), 2.0, A.is_equal, A.mult, ["lane"], ["isb%d" % t])
-    ts(T.hold[:], T.m16[:], cf(LANE), -BIG, A.is_le, A.mult, ["m16", "lane"], ["hold"])
-    ts(T.pick16[:], T.m16[:], cf(LANE), None, A.is_equal, None, ["m16", "lane"], ["pick16"])
-    ts(T.idn[:], T.dif[:], 0.0, None, A.is_equal, None, ["dif"], ["idn"])
-    ts(T.pois[:], T.hold[:], -2.0, -BIG, A.mult, A.add, ["hold"], ["pois"])
-    ts(T.keep16[:], T.m16[:], 0.5, None, A.is_gt, None, ["m16"], ["keep16"])
-    ts(cf(KTMP), cf(GE5), cf(GE7), cf(GE9), A.add, A.add, ["ge%d" % GE5, "ge%d" % GE7, "ge%d" % GE9], ["ktmp"])
-    for t in range(R - 1):
-        ts(cf(KADD + t), cf(ISB + t), -float(144 + B), cf(GE5 + t), A.mult, A.subtract, ["isb%d" % t, "ge%d" % (GE5 + t)], ["kadd%d" % t])
-    act(T.ze[:, 3:515:4], T.idn[:], F.Identity, ["idn", "par0"], ["ze"], scale=cf(PAR0))
-    act(T.zo[:, 3:515:4], T.idn[:], F.Identity, ["idn", "lane"], ["zo"], scale=cf(PAR1))
+    load("a", v("ub"), T.u[:], "ldu")
+    load("s", pages(0, HEAD), T.x[:, 0:4 * HEAD], "ldx")
+    load("s", pages(HEAD, C), T.x[:, 4 * HEAD:4 * C], "ldy")
+    load("s", raw(v("qw")), T.wc[:], "ldw", [pages(HEAD, C)])
+    load("s", v("sw"), T.ws[:], "lds")
+    load("s", v("vb"), T.v[:], "ldv")
 
     def tile_zero(k):
-        lo = min(16 * c for c in range(2, 25) if SLOT[c][0] == k)
-        zeros(T["tl%d" % k][:, 4 * lo:4 * TW[k]], 4 * (TW[k] - lo), ["tl%d_%d" % (k, s) for s in range(4)])
+        fill(v("tl%d" % k, 64 * min(c for c in range(2, 25) if SLOT[c][0] == k)))
 
-    for k in range(3):
+    iota(pi(0), [[0, 1]], 0, 1, True)
+    iota(v("pi", 16, 24), [[16, 8]], 0, 0, True)
+    iota(v("m16"), [[0, 25], [1, 16]], 0, 0)
+    iota(v("k0", 0, 25), [[16, 25]], 0, 0)
+    iota(v("dif"), [[1, 128]], 0, -1)
+    tile_zero(5)
+    tile_zero(0)
+    tile_zero(4)
+    iota(v("dg"), [[1, 8], [0, 64]], 0, 0)
+    for k in (2, 1, 3):
         tile_zero(k)
-    ts(col(KEY), cf(KTMP), cf(LLAB), 2.0 * (B + 144), A.add, A.add, ["ktmp", "llab"], ["key"])
-    ms(T.srt[:, C:464], FAR, ["srt1"])
-    ms(T.rs[:, V_LO:V_HI + 1], 128.0, ["rsv"])
-    quant(T.qu0[:], T.su0[:], T.ub[:], ["ub"], ["qu0"])
-    unit(0, 0)
-    cp(T.qu[:].bitcast(dt.uint32), T.qu0[:].bitcast(dt.uint32).indirect(T.uo[:]), ["qu0", "uo"], ["qu"])
-    act(T.su[:], T.su0[:].indirect(T.uo[:]), F.Copy, ["qu0", "uo"], ["su"])
-    for k in range(3, 6):
-        tile_zero(k)
-    unit(0, 1)
-    unit(1, 0)
-    unit(1, 1)
-    ts(T.zb[:], T.dg[:], cf(GRP), None, A.is_equal, None, ["dg", "lane"], ["zb"])
-    quant(T.qx0[:, 0:200], T.sx0[:, 0:200], T.st0[:, 0:800], ["xa"], ["qxa0"])
-    ts(T.cross[:], T.d2[:], cf(PAR1), FAR, A.not_equal, A.mult, ["d2", "lane"], ["cross"])
-    quant(T.qo[:], T.so[:], T.zb[:], ["zb"], ["qo"])
-    quant(T.qx0[:, 200:402], T.sx0[:, 200:402], T.st0[:, 800:YO], ["xb", "z0"], ["qxb0"])
-    plus(T.kc[:, 1:25], T.k0[:, 1:25], cf(LANE), ["k0", "lane"], ["kc"])
-    plus(T.kc[:, 0:1], cf(LANE), 16.0, ["lane"], ["kc0"])
-    plus(cf(LHALF), cf(LANE), 0.5, ["lane"], ["lhalf"])
-    plus(cf(TH0), cf(LANE), 0.5, ["lane"], ["th0"], -512.0)
-    plus(cf(TH1), cf(LANE), 0.5 - 512.0, ["lane"], ["th1"], -512.0)
-    plus(cf(LPOS4), cf(LANE), 240.0 + 48.0, ["lane"], ["lpos4"])
-    plus(cf(LPOS3), cf(LANE), 240.0 + 32.0, ["lane"], ["lpos3"])
-    plus(cf(T1348), cf(TQ), 1348.0, ["lane"], ["t1348"])
-    plus(T.kk[:, 0:4], T.k0[:, 0:4], cf(LHALF), ["k0", "lhalf"], ["kk"])
-    zeros(T.eb[:, 0:2], 2, ["eb0"])
-    plus(T.base[:], T.cross[:], col(KEY), ["cross", "key"], ["base"])
-    plus(T.pg4[:], T.pg0[:], cf(LANE), ["pg0", "lane"], ["pg4"])
+    iota(v("pay0"), [[int(STEP) + 4 * B, 5], [4, B]], int(STEP) * SLOT0, 0)
+    fill(v("rs", V_LO, 25), 128)
+    iota(v("d2"), [[1, 2], [0, 16]], 0, 0)
+    iota(v("m4"), [[0, 20], [1, 4]], 0, 0)
+    iota(v("lc", 32, 57), [[1, 5], [0, 5]], 0, 0)
+    fill(col(CNT), 2 * B)
+    fill(v("srt", C), 10 ** 6)
+    fill(v("dx", SPARE))
+    fill(v("sb", 256))
+    fill(v("tt", 4 * B))
+
+    def unit(b):
+        quant("qe", "se", 128 * b, 128 * b + 128, v("ze", 3 - b, 515 - b))
+
+    ts(pi(8), pi(0), 15, None, A.bitwise_and)
+    ts(pi(9), pi(0), 4, None, A.arith_shift_right)
+    ts(pi(10), pi(0), 4, 1, A.arith_shift_right, A.bitwise_and)
+    ts(pi(11), pi(0), 2, 3, A.arith_shift_right, A.bitwise_and)
+    ts(pi(12), pi(0), 3, None, A.bitwise_and)
+    cp(v("uo"), v("pi", 16, 24))
+    cp(v("cf", 0, 5), v("pi", 8, 13))
+    ms(v("ze"), 0.0)
+    ts(v("hold"), v("m16"), cf(LANE), -BIG, A.is_le, A.mult)
+    ts(v("kq"), v("m16"), 0.5, -2048.0, A.is_gt, A.mult)
+    quant("qu0", "su0", 0, 128, v("ub"))
+    ts(v("ze", 3, 515, 4), v("dif"), 0.0, None, A.is_equal)
+    cp(words(v("qu")), by(words(v("qu0")), v("uo")))
+    ts(v("kq", 0, C, 16), v("k0", 0, 25), cf(LANE), None, A.add)
+    unit(0)
+    ts(v("kq", 0, 1), cf(LANE), 16.0, None, A.add)
+    quant_x(0, HEAD)
+
+    plus(cf(LABL), cf(LANE), SLOT0 / 128.0, 1.0 / 128)
+    plus(cf(TH0), cf(LANE), 0.5 - STEP * SLOT0, -STEP)
+    plus(cf(TH1), cf(LANE), 0.5 - STEP * (SLOT0 + 1), -STEP)
+    plus(cf(LHALF), cf(LANE), 0.5)
+    plus(cf(KC), cf(LQ), 1.5, 2.0)
+    plus(v("pois"), v("hold"), -BIG, -2.0)
+    act(v("su"), by(v("su0"), v("uo")), F.Copy)
+    act(v("ab"), v("m16"), F.Abs, bias=cf(LANE), scale=-1.0)
+    act(v("keep16"), v("m16"), F.Sign)
+    act(v("pick16"), v("ab"), F.Relu, bias=1.0, scale=-1.0)
+
+    def keys(t):
+        plus(col(LGF), col(LG), cf(FARS + t))
+        plus(col(KEY2), col(CNT), col(LGF))
+        plus(col(KEY1), col(KEY2), cf(LABL))
+        plus(v("base", 32, 64), v("cross"), col(KEY2))
+        plus(v("base", 0, 32), v("cross"), col(KEY1))
+
+    def late_constants():
+        act(cf(LG0), cf(LANE), F.Relu, bias=-0.625, scale=0.125)
+        plus(cf(PFAR), cf(PAR), 0.0, -FAR)
+        for t in range(R):
+            act(cf(FARS + t), cf(LANE), F.Relu, bias=-(4.0 + t) * FAR, scale=FAR)
+        plus(col(LG), cf(LANE), cf(LG0), 0.125)
+        act(v("cross"), v("d2"), F.Abs, bias=cf(PFAR), scale=FAR)
+        act(v("ab", 0, B), v("m4"), F.Abs, bias=cf(LQ), scale=-1.0)
+        keys(0)
+        act(v("pick4"), v("ab", 0, B), F.Relu, bias=1.0, scale=-1.0)
+        act(v("keep4"), v("m4"), F.Sign)
+        plus(v("kk"), v("k0", 0, 4), cf(LHALF))
+
+    def last_constants():
+        plus(v("own"), v("k0", 0, 16), cf(LANE))
+        plus(v("kc2"), v("k0", 0, 16), cf(KC), 0.5)
+        plus(v("dum"), v("own"), float(SPARE))
+        plus(cf(PAR16), cf(PAR), 0.0, 16.0)
+        for t in range(R):
+            plus(cf(LNEW + t), cf(PAR), 5.0 + t, 16.0)
+        plus(v("lc", 0, 25), v("lc", 32, 57), cf(PAR16))
 
     def slot(c, n0, n1):
         k, s = SLOT[c]
-        return T["tl%d" % k][:, 4 * n0 + s:4 * n1:4], "tl%d_%d" % (k, s)
+        return v("tl%d" % k, 4 * n0 + s, 4 * n1, 4)
 
     def score(c):
-        return T.scn[:, 16 * c + 15:16 * c + 16], "scn_hi" if 16 * c >= HI else "scn_lo"
+        return v("scn", 16 * c + 15, 16 * c + 16)
 
     def rsum(c):
-        return T.rs[:, c:c + 1]
+        return v("rs", c, c + 1)
 
     qoff = [sum(TW[:k]) for k in range(6)]
 
     def tile_sum(k, start, stop):
-        a, b = qoff[k], qoff[k] + TW[k]
-        mx(2, TW[k], T.qo[:], T.so[:], T.qc[:, a:b], T.sc[:, a:b], ["qo", "qc%d" % k], start, stop)
+        quant("qc", "sc", qoff[k], qoff[k] + TW[k], v("tl%d" % k))
+        mx(2, QO, ("qc", "sc", qoff[k], qoff[k] + TW[k]), start, stop)
 
-    def tile_quant(k):
-        a, b = qoff[k], qoff[k] + TW[k]
-        quant(T.qc[:, a:b], T.sc[:, a:b], T["tl%d" % k][:], ["tl%d_%d" % (k, s) for s in range(4)], ["qc%d" % k])
-
-    def layer(bank0, q, s, rd):
+    def layer(bank0, x):
         for b in range(4):
-            mx(bank0 + b, 128, T.qw[:, 128 * b:128 * b + 128], T.sw[:, 128 * b:128 * b + 128], q, s, ["qw"] + rd)
+            mx(bank0 + b, ("qw", "sw", 128 * b, 128 * b + 128), x)
 
-    xkeys = ["xa", "xb"]
+    def unpack(b):
+        mx(4 + b, ("qe", "se", 128 * b, 128 * b + 128), ("qx", "sx", 0, C))
+
+    q1, q2, r2 = v("er", 15, C, 16), v("rr", 0, 25), v("rr", 32, 57)
+
+    def slots(t, step):
+        if step == 0:
+            ts(v("lc", 32, 57), r2, B - 0.5, cf(LNEW + t), A.is_lt, A.mult)
+        else:
+            tt(v("lc", 0, 25), v("lc", 0, 25), v("lc", 32, 57), A.max)
 
     for t in range(R):
-        st, qx, sx = T["st%d" % t], T["qx%d" % t], T["sx%d" % t]
-        qxk = ["qxa%d" % t, "qxb%d" % t]
-        nk, ns, l1, l2 = NK[t], NS[t], 5 + 2 * t, 6 + 2 * t
+        nk, ns = NK[t], NS[t]
 
-        mx(0, C, T.qu[:], T.su[:], qx[:, 0:C], sx[:, 0:C], ["qu", "su"] + qxk)
-        mx(1, C, T.qu[:], T.su[:], qx[:, 0:C], sx[:, 0:C], ["qu", "su"] + qxk)
+        mx(3, QU, ("qx", "sx", 0, HEAD))
+        quant_x(HEAD, C)
+        mx(0, QU, ("qx", "sx", 0, C))
+        mx(1, QU, ("qx", "sx", 0, 16 * max(ON_S)))
+        tt(v("rowp", 0, HEAD), v("p3", 0, HEAD), v("pois", 0, HEAD), A.min)
         if t == 0:
-            unit(2, 0)
-            unit(2, 1)
+            unit(1)
         else:
-            blank(t)
-        tt(T.rowp[:, HI:C], T.p0[:, HI:C], T.pois[:, HI:C], A.min, ["p0", "pois"], ["rowp_hi"])
-        tt(T.rowp[:, 0:HI], T.p0[:, 0:HI], T.pois[:, 0:HI], A.min, ["p0", "pois"], ["rowp_lo"])
-        scan(T.scn[:, HI:C], T.hold[:, HI:C], T.rowp[:, HI:C], 0.0, A.add, A.max, ["hold", "rowp_hi"], ["scn_hi"])
-        scan(T.scn[:, 0:HI], T.hold[:, 0:HI], T.rowp[:, 0:HI], 0.0, A.add, A.max, ["hold", "rowp_lo"], ["scn_lo"])
+            slots(t - 1, 0)
+        scan(v("scn", 0, HEAD), v("hold", 0, HEAD), v("rowp", 0, HEAD), 0.0, A.add, A.max)
+        if t == 0:
+            unit(2)
+            unit(3)
+        else:
+            slots(t - 1, 1)
+        for b in range(4):
+            unpack(b)
+        tt(v("rowp", HEAD, C), v("p0", HEAD, C), v("pois", HEAD, C), A.min)
+        scan(v("scn", HEAD, C), v("hold", HEAD, C), v("rowp", HEAD, C), 0.0, A.add, A.max)
+
+        jobs = [(0, 16, 32), (1, 0, 16)] + [(c, 0, 16 * c) for c in ON_S]
 
         def sign(i):
-            c = ON_S[i]
-            s, k = score(c)
-            act(T["sg%d" % (i % 3)][:, 0:16 * c], T.p1[:, 0:16 * c], F.Sign, ["p1", k], ["sg%d" % (i % 3)], bias=s, scale=-1.0)
+            c, lo, hi = jobs[i]
+            act(v("sg%d" % (i % 3), 0, hi - lo), v("p3" if c < HEAD // 16 else "p1", lo, hi), F.Sign, bias=score(c), scale=-1.0)
 
         def positive(i):
-            c = ON_S[i]
-            o, k = slot(c, 0, 16 * c)
-            act(o, T["sg%d" % (i % 3)][:, 0:16 * c], F.Relu, ["sg%d" % (i % 3)], [k, "rs%d" % c], accum_out=rsum(c))
+            c, lo, hi = jobs[i]
+            sg = v("sg%d" % (i % 3), 0, hi - lo)
+            if c == 0:
+                act(v("ab", 0, 16), sg, F.Sign, bias=1.0, total=rsum(c))
+            else:
+                act(v("ab", 16, 32) if c == 1 else slot(c, lo, hi), sg, F.Relu, total=rsum(c))
 
         sign(0)
-        for i in range(len(ON_S)):
-            if i + 1 < len(ON_S):
+        for i in range(len(jobs)):
+            if i + 1 < len(jobs):
                 sign(i + 1)
             positive(i)
-
-        def compare(c):
-            s, k = score(c)
-            o, ko = slot(c, 0, 16 * c)
-            ts(o, T.p0[:, 0:16 * c], s, None, A.is_lt, None, ["p0", k], [ko])
-
-        def along(c):
-            d0, k = slot(c, 0, 8 * c)
-            d1, k = slot(c, 8 * c, 16 * c)
-            e = 144 * (c - V_LO + 1)
-            scan(T.rh[:, e - 8 * c:e], d0, d1, -128.0, A.add, A.add, [k], ["rs%d" % c])
-
-        eo, ek = slot("E", 0, C)
-        ts(T.tiny[:, 0:16], T.p0[:, 16:32], score(0)[0], None, A.is_le, None, ["p0", "scn_lo"], ["tiny0"])
-        tt(eo, T.scn[:], T.p0[:, 0:C], A.is_ge, ["p0", "scn_lo", "scn_hi"], [ek])
-        ts(T.tiny[:, 16:32], T.p0[:, 0:16], score(1)[0], None, A.is_lt, None, ["p0", "scn_lo"], ["tiny1"])
-        compare(V_HI)
-        red(rsum(0), T.tiny[:, 0:16], A.add, ["tiny0"], ["rs0"])
-        red(rsum(1), T.tiny[:, 16:32], A.add, ["tiny1"], ["rs1"])
-        scan(T.er[:], T.keep16[:], eo, 0.0, A.mult, A.add, ["keep16", ek], ["er"])
-        for c in range(V_HI - 1, V_LO - 1, -1):
-            compare(c)
-            along(c + 1)
-            if c == 13:
-                tile_quant(2)
-            if c == 9:
-                tile_quant(0)
-                tile_sum(0, True, False)
-                tile_sum(2, False, False)
-                tile_quant(3)
-                tile_sum(3, False, False)
-        tt(q1, T.kc[:, 0:25], T.er[:, 15:C:16], A.subtract, ["kc", "kc0", "er"], ["q1"])
-        along(V_LO)
-        tile_quant(4)
-        tile_sum(4, False, False)
-        nv = V_HI - V_LO + 1
-        tt(T.rr[:, V_LO:V_HI + 1], T.rr[:, V_LO:V_HI + 1], T.rh[:, 143:144 * nv:144], A.subtract,
-           ["q1"] + ["rs%d" % c for c in range(V_LO, V_HI + 1)], ["q1"])
-        for k in (1, 5):
-            tile_quant(k)
-            tile_sum(k, False, k == 5)
-        tt(q2, q1, T.rs[:, 0:25], A.subtract, ["q1", "rsv"] + ["rs%d" % c for c in range(25)], ["q2"])
         if t == 0:
-            unit(3, 0)
-        tt(T.mm[:], T.p2[:, 0:C], T.pick16[:], A.mult, ["p2", "pick16"], ["mm"])
-        scan(T.dd[:], T.keep16[:], T.mm[:], 0.0, A.mult, A.add, ["keep16", "mm"], ["dd"])
-        tt(r2, T.dd[:, 15:C:16], q2, A.add, ["dd", "q2"], ["r2"])
-        rk = T.rk[:, 0:25]
-        cp(rk, r2, ["r2"], ["rk"])
-
-        cp(T.srt[:, 0:C].indirect(rk), T.pay[:], ["rk", "pay"], ["srt"])
-        act(T.sg0[:, 0:B], T.srt[:, 0:B], F.Sign, ["srt", "th0"], ["sg0", "s0"], bias=cf(TH0), accum_out=col(S0))
-        act(T.sg1[:, 0:B], T.srt[:, 0:B], F.Sign, ["srt", "th1"], ["sg1", "s1"], bias=cf(TH1), accum_out=col(S1))
-        act(T.lab[:], T.srt[:, B:C], F.Identity, ["srt"], ["lab"], scale=1.0 / 4096, bias=(LAB0 - 0.39) / 8)
-        ts(T.lt[:], T.srt[:, 0:B], 1.0 / 512, LAB0 - 0.39, A.mult, A.add, ["srt"], ["lt"])
-        plus(a80, T.lt[:], 512.0 * LAB0, ["lt"], ["a80"], -512.0)
-        ts(T.kr[:], T.base[:], col(S0), col(S1), A.subtract, A.add, ["base", "s0", "s1"], ["kr"])
-        op("v", lambda: g.vector.transpose(T.kt[:], T.kr[:]), ["kr"], ["kt"])
-        red(col(VMIN), T.kt[:], A.min, ["kt"], ["vmin"])
-        cs, cl = T.cs[:, 8 * t:8 * t + 1], T.cl[:, 8 * t:8 * t + 1]
-        ts(cs, col(VMIN), 0.5, -8.31, A.mult, A.add, ["vmin"], ["cs%d" % t])
-        send(cl, cs, "cnt%d" % t, ["cs%d" % t])
-        ts(col(VV), cs, -2.0, col(VMIN), A.mult, A.add, ["cs%d" % t, "vmin"], ["vv"])
-
-        ts(T.ea[:], T.lab[:], col(VV), 145.0, A.is_equal, A.mult, ["lab", "vv"], ["ea"])
-        ts(T.eb[:, 2:322], T.lab[:], col(VV), 144.0, A.is_equal, A.mult, ["lab", "vv"], ["eb"])
-        plus(col(V512), col(VV), -512.0 * LAB0, ["vv"], ["v512"], 4096.0)
-        plus(col(DCOL), col(VV), 512.0 * (LAB0 + l2), ["vv"], ["dcol"], -4096.0)
-        scan(T.zw[:, B:C], T.ea[:], T.eb[:, 1:321], 0.0, A.add, A.subtract, ["ea", "eb", "eb0"], ["zw"])
-
-        on_v = range(nk - 2)
-        for k in (nk - 1, nk - 2):
-            lo, sg = B - 32 * (nk - 1 - k), "sg%d" % (k % 2)
-            act(T[sg][:, 0:C - lo], T.zw[:, lo:C], F.Sign, ["zw", "zw0", "kk"], ["pb%d" % k, sg],
-                bias=T.kk[:, k:k + 1], scale=-1.0, accum_out=T.pb[:, 160 * k + 159:160 * k + 160])
-        for k in on_v:
-            ts(T.le[:, 320 * k:320 * k + 320], T.zw[:, B:C], T.kk[:, k:k + 1], 2.0, A.is_lt, A.mult, ["zw", "kk"], ["le%d" % k])
-        for k in on_v:
-            scan(T.pb[:, 160 * k:160 * k + 160], T.le[:, 320 * k:320 * k + 160], T.le[:, 320 * k + 160:320 * k + 320],
-                 -320.0 - 32.0 * (nk - 1 - k), A.add, A.add, ["le%d" % k], ["pb%d" % k])
-        if nk == 3:
-            tt(g80, T.srt[:, 0:B], a80, A.add, ["srt", "a80"], ["g80"])
-        pbk = ["pb%d" % k for k in range(nk)]
-        lp = cf(LPOS4 if nk == 4 else LPOS3)
-        for h in range(2):
-            ts(T.pos[:, h:2 * nk:2], T.pb[:, 159:160 * nk:160], 0.5, lp, A.mult, A.add, pbk + ["lpos4", "lpos3"], ["pos%d" % h])
-        ts(T.sv1[:, 0:32 * nk], T.srt[:].indirect(T.pos[:, 0:2 * nk]), col(V512), float(C), A.subtract, A.min,
-           ["srt", "srt1", "pos0", "pos1", "v512"], ["sv1"])
-        op("v", lambda: g.vector.transpose(T.sv2[:, 0:32 * nk], T.sv1[:, 0:32 * nk]), ["sv1"], ["sv2"])
-        cp(T.po[:, 0:nk], T.sv2[:, 0:32 * nk:32], ["sv2"], ["po0"])
-        cp(T.po[:, nk:2 * nk], T.sv2[:, 16:32 * nk:32], ["sv2"], ["po1"])
-        po = T.po[:, 0:2 * nk]
-        qp, sp = T["qp%d" % t], T["sp%d" % t]
-        cp(qp[:, 0:32 * nk].bitcast(dt.uint32), qx[:].bitcast(dt.uint32).indirect(po), qxk + ["po0", "po1"], ["qp%d" % t])
-        act(sp[:, 0:32 * nk], sx[:].indirect(po), F.Copy, qxk + ["po0", "po1"], ["sp%d" % t])
-        if t == 0:
-            unit(3, 1)
-        w = 16 * nk
+            plus(v("pay"), v("pay0"), cf(TQ))
         for b in range(4):
-            rd = ["qp%d" % t, "sp%d" % t, "qe%d" % (2 * b), "qe%d" % (2 * b + 1)]
-            e0, e1 = 256 * b, 256 * b + 128
-            mx(4 + b, 128, T.qe[:, e0:e0 + 128], T.se[:, e0:e0 + 128], qp[:, 0:128], sp[:, 0:128], rd, True, False)
-            mx(4 + b, 128, T.qe[:, e1:e1 + 128], T.se[:, e1:e1 + 128], qp[:, w:w + 128], sp[:, w:w + 128], rd, False, True)
-
+            act(v("dx", b, 4 * C, 4), v("p%d" % (4 + b), 0, C), F.Copy)
         if t == 0:
-            ts(T.pick4[:], T.m4[:], cf(LQ), None, A.is_equal, None, ["m4", "lane"], ["pick4"])
+            late_constants()
+
+        eo = slot("E", 0, C)
+        tt(eo, v("scn"), v("p0", 0, C), A.is_ge)
+        if t == 0:
+            ts(v("zb"), v("dg"), cf(GRP), None, A.is_equal)
+        tiles = [c for c in V_PLAN if isinstance(c, str) and c[0] == "q"]
+        for c in V_PLAN:
+            if c == "er":
+                scan(v("er"), v("kq"), eo, -2048.0, A.max, A.subtract)
+            elif c in tiles:
+                if t == 0 and c == tiles[0]:
+                    quant("qo", "so", 0, 128, v("zb"))
+                tile_sum(int(c[1]), c == tiles[0], c == tiles[-1])
+            elif c > 0:
+                ts(slot(c, 0, 16 * c), v("p0", 0, 16 * c), score(c), None, A.is_lt)
+            else:
+                e = 192 * (1 - c - V_LO)
+                scan(v("rh", e + 8 * c, e), slot(-c, 0, -8 * c), slot(-c, -8 * c, -16 * c), -128.0, A.add, A.add)
+        tt(q2, q1, v("rs", 0, 25), A.subtract)
+        tt(v("rr", V_LO, 25), v("rr", V_LO, 25), v("rh", 191, None, 192), A.subtract)
+        tt(v("mm"), v("p2", 0, C), v("pick16"), A.mult)
+        scan(v("dd"), v("keep16"), v("mm"), 0.0, A.mult, A.add)
+        tt(r2, v("dd", 15, C, 16), q2, A.add)
+        rk = v("rk", 0, 25)
+        cp(rk, r2)
+
+        cp(by(v("srt", 0, C), rk), v("pay"))
+        top = v("srt", 0, B)
+        act(v("sg0", 0, B), top, F.Sign, bias=cf(TH0), total=col(S0))
+        act(v("sg1", 0, B), top, F.Sign, bias=cf(TH1), total=col(S1))
+        plus(v("lab"), v("srt", B, C), -800.0 / FINE, 1.0 / FINE)
+        ts(v("lt"), top, -800.0, None, A.add)
+        tt(g80, top, v("lt"), A.subtract)
+        ts(v("kr"), v("base"), col(S0), col(S1), A.subtract, A.add)
+        turn(v("kt"), v("kr"))
+        red(col(VM2), v("kt", 32, 64), A.min)
+        red(col(VM1), v("kt", 0, 32), A.min)
+        cs, cl = v("cs%d" % t, 0, 1), v("cl%d" % t, 0, 1)
+        plus(cs, col(VM2), 0.0, -FINE)
+        send(cl, cs, "cnt%d" % t)
+        plus(col(VV), col(VM1), cs, FINE)
+
+        ts(v("ind"), v("lab"), col(VM2), col(VM1), A.add, A.is_equal)
+        scan(v("cnt"), v("ind"), v("ind"), 0.0, A.add, A.max)
+        for k in range(1, nk):
+            act(v("sg%d" % (k % 2), 0, 304), v("cnt", 16, 320), F.Sign, bias=v("kk", k, k + 1), scale=-1.0,
+                total=v("pb", 160 * k + 159, 160 * k + 160))
+        ts(v("le"), v("cnt"), v("kk", 0, 1), 2.0, A.is_lt, A.mult)
+        tt(h80, g80, v("pick4"), A.mult)
+        scan(v("pb", 0, 160), v("le", 0, 160), v("le", 160, 320), -336.0, A.add, A.add)
+        scan(i80, v("keep4"), h80, 0.0, A.mult, A.add)
+
+        def relabel():
+            ts(col(CNT), col(CNT), col(S0), col(S1), A.subtract, A.add)
+            ts(col(ISV), col(CNT), col(LGF), col(VM2), A.add, A.is_equal)
+            ts(col(LG), col(ISV), (6 + 2 * t) / 8.0, col(LG), A.mult, A.max)
+
+        cp(v("to"), v("w80", 2 * B + 3, 3 * B, 4))
+        act(v("tt", 0, 4 * B), by(pages(0, C), v("to")), F.Copy)
         if nk == 4:
-            tt(g80, T.srt[:, 0:B], a80, A.add, ["srt", "a80"], ["g80"])
+            relabel()
+        w = 16 * nk
+        ts(v("pos", 0, nk), v("pb", 159, 160 * nk, 160), 0.5, 248.0, A.mult, A.add)
+        tt(v("xg", 0, w), by(v("srt"), v("pos", 0, nk)), v("pick4", 0, w), A.mult)
+        scan(v("xs", 0, w), v("keep4", 0, w), v("xg", 0, w), 0.0, A.mult, A.add)
+        xs = v("xs", 3, w, 4)
+        ts(v("gl", 0, 4 * nk), xs, col(VV), float(SPARE), A.subtract, A.min)
+
+        act(v("sb", 2 * w, 4 * w), by(v("dx"), v("gl", 2 * nk, 4 * nk)), F.Copy)
+        cp(v("sb", 0, 2 * w), by(v("dx"), v("gl", 0, 2 * nk)))
+        qs, ss, qt, sq = "qs%d" % t, "ss%d" % t, "qt%d" % t, "sq%d" % t
+        quant(qs, ss, 0, 128, v("sb"))
+        send(raw(v(qt, 128, 128 + ns)), raw(v(qs, 0, ns)), "arr%d" % t)
+        send(v(sq, 128, 128 + ns), v(ss, 0, ns), "arr%d" % t)
+
+        quant(qt, sq, 0, 128, v("tt"))
+        layer(0, (qt, sq, 0, 128))
         if t == 0:
-            ts(T.keep4[:], T.m4[:], 0.5, None, A.is_gt, None, ["m4"], ["keep4"])
-        tt(h80, g80, T.pick4[:, 0:B], A.mult, ["g80", "pick4"], ["h80"])
-        if t > 0:
-            ts(T.ec[:], T.lab[:], col(VV), col(DCOL), A.is_equal, A.mult, ["lab", "vv", "dcol"], ["ec"])
-
+            last_constants()
+        off = v("off", 0, 4 * nk)
+        ts(off, xs, col(VV), None, A.subtract)
+        if nk < 4:
+            relabel()
+        tt(v("slf", 0, 4 * nk), off, v("dum", 0, 4 * nk), A.min)
+        cp(v("sl", 0, 4 * nk), v("slf", 0, 4 * nk))
+        landed([cl], "cnt%d" % t, n_in)
+        hm = [v("hm", 16 * k, 16 * k + 4 * nk) for k in range(3)]
+        act(hm[0], v("kc2", 0, 4 * nk), F.Sign, bias=cl, scale=FINE)
+        if t + 1 < R:
+            plus(top, g80, STEP * (SLOT0 + 5 + t))
+        plus(hm[1], hm[0], 128.0, -128.0)
         for b in range(4):
-            act(st[:, SO + b:SO + 4 * w:4], T["p%d" % (4 + b)][:, 0:w], F.Copy, ["p%d" % (4 + b)], ["S%d_%d" % (t, b)])
-        scan(i80, T.keep4[:, 0:B], h80, 0.0, A.mult, A.add, ["keep4", "h80"], ["i80"])
-        ts(T.to[:], T.w80[:, 3 * B + 3:4 * B:4], 4.0, cf(TQ), A.mult, A.add, ["i80", "lane"], ["to"])
-        qs, ss, qt, sq = T["qs%d" % t], T["ss%d" % t], T["qt%d" % t], T["sq%d" % t]
-        quant(qs[:], ss[:], st[:, HO:END], hs_keys[t], ["qs%d" % t])
-        send(qt[:, 128:128 + ns].bitcast(dt.uint8), qs[:, 64:64 + ns].bitcast(dt.uint8), "arr%d" % t, ["qs%d" % t])
-        send(sq[:, 128:128 + ns], ss[:, 64:64 + ns], "arr%d" % t, ["qs%d" % t])
+            act(v("yt", b, 4 * B, 4), v("p%d" % b, 0, B), F.Copy, scale=0.03125)
+        tt(hm[2], hm[1], v("own", 0, 4 * nk), A.add)
+        if t + 1 == R:
+            slots(t, 0)
+            quant("qv", "sv", 0, 128, v("vb"))
+            slots(t, 1)
+        cp(v("hl", 0, 4 * nk), hm[2])
+        if t + 1 < R:
+            act(v("pay"), by(v("srt", 0, C), rk), F.Copy)
+        else:
+            plus(v("tb", 0, 32), v("cross"), col(LG), 0.0)
+            cp(v("lu", 0, 25), v("lc", 0, 25))
+            turn(v("tb", 32, 64), v("tb", 0, 32))
+            act(v("lf"), by(v("tb", 32, 64), v("lu", 0, 25)), F.Copy, scale=8.0)
+            store("a", T.ob[:], (T.lf[0:128:16, :], v("lf")[1]))
+        cp(by(v("st"), v("to")), v("yt"))
 
-        act(T.tt[:, 0:4 * B], st[:, 0:1600].indirect(T.to[:]), F.Copy, xkeys + ["to"], ["tt"])
-        tt(T.zm[:], T.zw[:].indirect(rk), T.pick4[:], A.mult, ["zw", "zw0", "rk", "pick4"], ["zm"])
-        quant(qt[:, 0:128], sq[:, 0:128], T.tt[:], ["tt", "ttz"], ["qt%d" % t])
-        layer(0, qt[:, 0:128], sq[:, 0:128], ["qt%d" % t, "sw"])
-        scan(T.zs[:], T.keep4[:], T.zm[:], 0.0, A.mult, A.add, ["keep4", "zm"], ["zs"])
-        if t == 0:
-            ts(T.ec[:], T.lab[:], col(VV), col(DCOL), A.is_equal, A.mult, ["lab", "vv", "dcol"], ["ec"])
-        z = T.zs[:, 3:C:4]
-        plus(T.sn[:, 0:B], g80, 512.0 * l1, ["g80"], ["sn0"])
-        plus(cc[1], z, cf(T1348), ["zs", "t1348"], ["c2"], 4.0)
-        ts(cc[0], z, 64.5, -4096.0, A.is_lt, A.mult, ["zs"], ["c1"])
+        landed([v(qt, 128, 128 + ns), v(sq, 128, 128 + ns)], "arr%d" % t, 2 * n_in)
+        layer(4, (qt, sq, ns, 128 + ns))
         for b in range(4):
-            act(st[:, YO + b:HO:4], T["p%d" % b][:, 0:B], F.Copy, ["p%d" % b], ["Y%d_%d" % (t, b)], scale=0.03125)
-        wrote["cl%d" % t] = ("cnt%d" % t, n_in, {}, "r")
-        ts(cc[4], z, cl, 256.0, A.is_gt, A.mult, ["zs", "cl%d" % t], ["c5"])
-        tt(cc[2], cc[0], cc[1], A.add, ["c1", "c2"], ["c3"])
-        nx, u = T["st%d" % (t + 1)], t + 1
-        if u < R:
-            ts(col(GG), cf(LLAB), col(VV), FAR, A.is_equal, A.mult, ["llab", "vv"], ["gg"])
-        tt(cc[3], cc[2], T.pg4[:], A.max, ["c3", "pg4"], ["c4"])
-        tt(cc[5], cc[3], cc[4], A.add, ["c4", "c5"], ["c6"])
-        cp(T.eo[:], cc[5], ["c6"], ["eo"])
-        tt(T.sn[:, B:C], T.srt[:, B:C], T.ec[:], A.add, ["srt", "ec"], ["sn"])
-        if u == R:
-            quant(T.qv[:], T.sv[:], T.vb[:], ["vb"], ["qv"])
-            act(T.pay[:], T.sn[:].indirect(rk), F.Copy, ["sn", "sn0", "rk"], ["pay"])
+            act(v("sb", 256 + b, 256 + 4 * ns, 4), v("p%d" % (4 + b), 128 - ns, 128), F.Copy, scale=0.03125)
+        act(v("zt", 2 * w, 4 * w), by(v("sb"), v("hl", 2 * nk, 4 * nk)), F.Copy)
+        cp(v("zt", 0, 2 * w), by(v("sb"), v("hl", 0, 2 * nk)))
+        cp(by(v("st"), v("sl", 0, 4 * nk)), v("zt", 0, 4 * w))
+        if t + 1 < R:
+            keys(t + 1)
+            quant_x(0, HEAD)
 
-        wrote["land%d" % t] = ("arr%d" % t, 2 * n_in, {}, "r")
-        layer(4, qt[:, ns:128 + ns], sq[:, ns:128 + ns], ["qt%d" % t, "sw", "land%d" % t])
-        for b in range(4):
-            act(st[:, HO + b:HO + 4 * ns:4], T["p%d" % (4 + b)][:, 128 - ns:128], F.Copy, ["p%d" % (4 + b)], ["H%d_%d" % (t, b)], scale=0.03125)
-        every = xkeys + hs_keys[t] + ["z%d" % t, "eo"] + ["Y%d_%d" % (t, b) for b in range(4)]
-        xkeys = ["xa%d" % u, "xb%d" % u]
-        cp(nx[:, 0:800], st[:].indirect(T.eo[:, 0:50]), every, [xkeys[0]])
-        act(nx[:, 800:1600], st[:].indirect(T.eo[:, 50:100]), F.Copy, every, [xkeys[1]])
-        last = 402 if u < R else C
-        quant(T["qx%d" % u][:, 0:200], T["sx%d" % u][:, 0:200], nx[:, 0:800], [xkeys[0]], ["qxa%d" % u])
-        quant(T["qx%d" % u][:, 200:last], T["sx%d" % u][:, 200:last], nx[:, 800:4 * last], [xkeys[1], "z%d" % u], ["qxb%d" % u])
-        if u < R:
-            act(T.pay[:], T.sn[:].indirect(rk), F.Copy, ["sn", "sn0", "rk"], ["pay"])
-            act(col(K2), cs, F.Identity, ["cs%d" % t, "isb%d" % t, "kadd%d" % t], ["k2"], scale=cf(ISB + t), bias=cf(KADD + t))
-            plus(col(K1), col(S0), col(KEY), ["s0", "key"], ["k1"], -1.0)
-            plus(col(K3), col(GG), col(K2), ["gg", "k2"], ["k3"])
-            plus(col(K4), col(S1), col(K1), ["s1", "k1"], ["k4"])
-            plus(col(KEY), col(K4), col(K3), ["k4", "k3"], ["key"])
-            plus(T.base[:], T.cross[:], col(KEY), ["cross", "key"], ["base"])
-
-    dma("s", T.oc[:, 0:800], T.qx3[:, 0:200].bitcast(dt.uint8), ["qxa3"], [], "out")
-    mx(0, 200, T.qv[:], T.sv[:], T.qx3[:, 0:200], T.sx3[:, 0:200], ["qv", "qxa3"])
-    dma("s", T.oc[:, 800:1600], T.qx3[:, 200:C].bitcast(dt.uint8), ["qxb3"], [], "out")
-    mx(1, 200, T.qv[:], T.sv[:], T.qx3[:, 200:C], T.sx3[:, 200:C], ["qv", "qxb3"])
-    act(T.yb[:, 0:200], T.p0[:, 0:200], F.Copy, ["p0"], ["ya"])
-    cp(T.yb[:, 200:C], T.p1[:, 0:200], ["p1"], ["yb"])
-    dma("a", T.y[:], T.yb[:], ["ya", "yb"], [], "out")
-    ts(T.er[:], T.pay[:], 1.0 / 512, LAB0 - 0.39, A.mult, A.add, ["pay"], ["er"])
+    quant_x(0, TAIL)
+    mx(0, QV, ("qx", "sx", 0, TAIL))
+    store("s", T.oc[:, 0:4 * TAIL], raw(v("qx", 0, TAIL)))
+    quant_x(TAIL, C)
+    mx(1, QV, ("qx", "sx", TAIL, C))
+    act(v("yb", 0, TAIL), v("p0", 0, TAIL), F.Copy)
+    cp(v("yb", TAIL, C), v("p1", 0, C - TAIL))
+    store("s", T.oc[:, 4 * TAIL:4 * C], raw(v("qx", TAIL, C)))
+    store("a", T.y[:, 0:TAIL], v("yb", 0, TAIL))
     for k in range(4):
-        dma("s", T.osc[4 * k:4 * k + 4, :], T.sx3[32 * k:32 * k + 4, :], ["qxa3", "qxb3"], [], "out")
-    ts(T.lf[:], T.er[:], -float(LAB0), None, A.add, None, ["er"], ["lf"])
-    dma("a", T.ob[:], T.lf[0:128:16, :], ["lf"], [], "out")
-    for sem in ("cv", "ca", "ct", "cg", "ldx", "ldy", "ldu", "ldw", "ldz", "loc", "out"):
-        g.wait_ge(T.sem[sem], count[sem])
+        store("s", T.osc[4 * k:4 * k + 4, :], (T.sx[32 * k:32 * k + 4, :], v("sx")[1]))
+    store("a", T.y[:, TAIL:C], v("yb", TAIL, C))
+    for sem in SEMAPHORES:
+        if sem in count:
+            g.wait_ge(T.sem[sem], count[sem])

@@ -6,15 +6,22 @@ NS = (64, 56, 48)
 BIG = 1e29
 FAR = 8192.0
 SPARE = 4 * C
+HO = SPARE + 256
 HEAD = 128
-TAIL = 272
+PIECES = ((0, 136), (136, 272), (272, C))
 TW = (400, 336, 272, 208, 144, 128)
 SLOT = {"E": (0, 0)}
 for _c in range(24, 1, -1):
     SLOT[_c] = ((25 - _c) // 4, (25 - _c) % 4)
+TILES = (0, 1, 5, 2, 3, 4)
+TOFF = {_k: sum(TW[_j] for _j in TILES[:TILES.index(_k)]) for _k in TILES}
 ON_S = (5, 4, 3, 2, 7, 6, 16, 15, 14, 13, 12, 11, 10, 9, 8)
 V_LO = 17
-V_PLAN = (24, 23, 22, "q0", 21, 20, "q5", 19, 18, "q1", 17, "er", "q2", -24, -23, -22, -21, "q3", -20, -19, -18, "q4", -17)
+V_PLAN = (24, 23, 22, 21, "q0", 20, 19, 18, 17, "q15", "er", "q2", -24, -23, -22, "q3", -21, -20, "q4", -19, -18, -17)
+PLAN = ("u u u u e e e s0 s1 lab lt g80 kr2 h80 turn i80 vm2 vm1 to take_t ind vv cnt pad search_s below quant_t search_v pos d late "
+        "xg xs gl y d d d off w2' top' pay' slot0 put_y slot1 ends take_s w2 top hm0 quant_s hm1 pay hm2 hl rest_y labels h take_z put_z "
+        "next").split()
+KN = {"nv": (2, 2, 2), "cut": 12, "sv": 1, "zv": 1}
 STEP = 2048.0
 SLOT0 = 129
 FINE = 128.0 * STEP
@@ -30,40 +37,44 @@ def _sb(name, n, d):
 for _k in range(8):
     SCRATCH["p%d" % _k] = ("psum", [128, 512], F32)
 for _t in range(R):
-    _sb("qs%d" % _t, 128, Q8); _sb("ss%d" % _t, 128, U8)
-    _sb("qt%d" % _t, 192, Q8); _sb("sq%d" % _t, 192, U8)
-    _sb("cs%d" % _t, 4, F32); _sb("cl%d" % _t, 4, F32)
-for _k in range(6):
-    _sb("tl%d" % _k, 4 * TW[_k], BF)
+    _sb("qr%d" % _t, C, Q8); _sb("sr%d" % _t, C, U8)
+    _sb("gl%d" % _t, 16, U16); _sb("gr%d" % _t, 16, U16)
+    if "u" not in PLAN:
+        _sb("qs%d" % _t, 128, Q8); _sb("ss%d" % _t, 128, U8)
+        _sb("cs%d" % _t, 4, F32); _sb("cl%d" % _t, 4, F32)
+for _t in range(R + 1):
+    _sb("qx%d" % _t, C, Q8); _sb("sx%d" % _t, C, U8)
 for _n, _w, _d in (
-        ("st", SPARE + 256, BF), ("dx", SPARE + 8, BF), ("qx", C, Q8), ("sx", C, U8), ("qc", 1488, Q8), ("sc", 1488, U8),
+        ("tl", 4 * sum(TW), BF), ("sg3", 384, BF),
+        ("st", SPARE + 256, BF), ("dx", HO + 256, BF), ("dy", HO, BF), ("qc", 1488, Q8), ("sc", 1488, U8),
+        ("qs", 128, Q8), ("ss", 128, U8), ("qt", 128, Q8), ("sq", 128, U8),
         ("ub", 512, BF), ("vb", 512, BF), ("qu0", 128, Q8), ("su0", 128, U8), ("qu", 128, Q8), ("su", 128, U8),
         ("qv", 128, Q8), ("sv", 128, U8), ("qw", 512, Q8), ("sw", 512, U8),
         ("qe", 512, Q8), ("se", 512, U8), ("qo", 128, Q8), ("so", 128, U8),
         ("ze", 520, BF), ("zb", 512, BF), ("tt", 512, BF), ("sb", 512, BF), ("yt", 320, BF), ("zt", 256, BF),
-        ("pi", 24, I32), ("cf", 32, F32), ("uo", 8, U16),
-        ("dif", 128, BF), ("dg", 512, BF), ("d2", 32, F32), ("m16", C, BF), ("m4", B, BF), ("ab", C, BF),
+        ("pi", 24, I32), ("cf", 16, F32), ("uo", 8, U16),
+        ("dif", 128, BF), ("dg", 128, BF), ("d2", 32, F32), ("m16", C, BF), ("m4", B, BF), ("ab", B, BF),
         ("hold", C, BF), ("pois", C, BF), ("pick16", C, BF), ("keep16", C, BF), ("kq", C, F16), ("pick4", B, BF), ("keep4", B, BF),
-        ("cross", 32, F32), ("k0", 32, F32), ("kk", 4, F32), ("kc2", 16, F32), ("own", 16, F32), ("dum", 16, F32), ("pay0", C, F32),
+        ("cross", 32, F32), ("k0", 32, F32), ("kk", 4, F32), ("own", 16, F32), ("kc2", 16, F32), ("dum", 16, F32), ("pay0", C, F32),
         ("rowp", C, F32), ("scn", C, F32), ("sg0", 384, BF), ("sg1", 384, BF), ("sg2", 384, BF),
-        ("rs", 32, F32), ("rh", 192 * (25 - V_LO), BF), ("er", C, F16), ("rr", 96, F32), ("mm", C, F16), ("dd", C, F16),
-        ("rk", 26, U16), ("pay", C, F32), ("srt", C + 8, F32),
+        ("rs", 32, F32), ("rh", 192 * 12, BF), ("er", C, F16), ("rr", 96, F32), ("mm", C, F16), ("dd", C, F16),
+        ("rk", 26, U16), ("pay", C, F32), ("srt", C + 64, F32),
         ("lt", B, BF), ("base", 64, F32), ("lab", 320, BF), ("col", 16, F32), ("kr", 64, F32), ("kt", 64, F32),
-        ("ind", 320, BF), ("cnt", 320, BF), ("le", 320, BF), ("pb", 640, F32),
-        ("pos", 4, U16), ("xg", 64, F32), ("xs", 64, F32), ("gl", 16, U16), ("off", 16, F32), ("slf", 16, F32), ("sl", 16, U16),
+        ("ind", 384, BF), ("cnt", 384, BF), ("le", 1344, BF), ("pb", 672, F32), ("pad0", 64, F32), ("pad", 64, F32),
+        ("pos", 4, U16), ("xg", 64, F32), ("xs", 64, F32), ("off", 16, F32),
         ("hm", 48, F32), ("hl", 16, U16), ("w80", 240, F32), ("to", 20, U16),
         ("lc", 64, F32), ("lu", 26, U16), ("tb", 64, F32), ("yb", C, F32), ("lf", C, F32)):
     _sb(_n, _w, _d)
 
 SEMAPHORES = (["cv", "ca", "ct", "cg", "ldu", "ldx", "ldy", "ldw", "lds", "ldv", "out", "loc"]
-              + ["cnt%d" % _t for _t in range(R)] + ["arr%d" % _t for _t in range(R)])
+              + ["lst%d" % _t for _t in range(R)] + ["arr%d" % _t for _t in range(R)])
 
-LANE, GRP, PAR, LQ, TQ, LABL, TH0, TH1, LHALF, KC, LG0, PFAR, PAR16 = range(13)
-FARS, LNEW = 16, 20
-S0, S1, VM1, VM2, VV, CNT, ISV, LG, LGF, KEY2, KEY1 = range(11)
+LANE, PAR, LQ, TQ, GRP, LABL, MINE, LHALF, LG0, PFAR, PAR16, LNEW, TH0, TH1 = range(14)
+W2, VF, VM1, VM2, VV, CNT, ISV, LG, LGF, KEY2, KEY1, S0, S1 = range(13)
 
 
 def rank_program(g, core, T, topo):
+    EARLY = "u" in PLAN
     rank = T.rank_of(core)
     if rank is None:
         return
@@ -220,8 +231,8 @@ def rank_program(g, core, T, topo):
     def pages(lo, hi):
         return v("st", 4 * lo, 4 * hi)
 
-    def quant_x(lo, hi):
-        quant("qx", "sx", lo, hi, pages(lo, hi))
+    def quant_x(t, lo, hi):
+        quant("qx%d" % t, "sx%d" % t, lo, hi, pages(lo, hi))
 
     QU, QV, QO = ("qu", "su", 0, 128), ("qv", "sv", 0, 128), ("qo", "so", 0, 128)
     g80, h80, i80 = [v("w80", B * k, B * k + B) for k in range(3)]
@@ -233,95 +244,97 @@ def rank_program(g, core, T, topo):
     load("s", v("sw"), T.ws[:], "lds")
     load("s", v("vb"), T.v[:], "ldv")
 
-    def tile_zero(k):
-        fill(v("tl%d" % k, 64 * min(c for c in range(2, 25) if SLOT[c][0] == k)))
+    def unwritten(k):
+        return v("tl", 4 * TOFF[k] + 64 * min(c for c in range(2, 25) if SLOT[c][0] == k), 4 * (TOFF[k] + TW[k]))
 
+    ms(v("ze"), 0.0)
     iota(pi(0), [[0, 1]], 0, 1, True)
-    iota(v("pi", 16, 24), [[16, 8]], 0, 0, True)
     iota(v("m16"), [[0, 25], [1, 16]], 0, 0)
+    one = v("ze", 3, 515, 4)
+    op("g", lambda: g.affine_select(one[0], one[0], [[1, 128]], A.not_equal, 1.0, 0, -1), [one], [one])
     iota(v("k0", 0, 25), [[16, 25]], 0, 0)
+    iota(v("pi", 16, 24), [[16, 8]], 0, 0, True)
     iota(v("dif"), [[1, 128]], 0, -1)
-    tile_zero(5)
-    tile_zero(0)
-    tile_zero(4)
-    iota(v("dg"), [[1, 8], [0, 64]], 0, 0)
-    for k in (2, 1, 3):
-        tile_zero(k)
+    for k in (5, 0, 4):
+        fill(unwritten(k))
+    iota(v("d2"), [[1, 2], [0, 16]], 0, 0)
+    fill(col(CNT), 2 * B)
+    iota(v("m4"), [[0, 20], [1, 4]], 0, 0)
     iota(v("pay0"), [[int(STEP) + 4 * B, 5], [4, B]], int(STEP) * SLOT0, 0)
     fill(v("rs", V_LO, 25), 128)
-    iota(v("d2"), [[1, 2], [0, 16]], 0, 0)
-    iota(v("m4"), [[0, 20], [1, 4]], 0, 0)
-    iota(v("lc", 32, 57), [[1, 5], [0, 5]], 0, 0)
-    fill(col(CNT), 2 * B)
-    fill(v("srt", C), 10 ** 6)
-    fill(v("dx", SPARE))
-    fill(v("sb", 256))
-    fill(v("tt", 4 * B))
+    iota(v("pad0"), [[4, 64]], SPARE, 0)
+    fill(v("ind", 320), 1)
+
+    def late_fills():
+        iota(v("keep16"), [[0, 25], [2048, 16]], 0, 0)
+        fill(v("tt", 4 * B))
+        iota(v("own"), [[16, 16]], HO, 0)
+        iota(v("lc", 32, 57), [[1, 5], [0, 5]], 0, 0)
+        fill(v("dy", SPARE))
+        fill(v("sb", 256))
+        fill(v("dx", SPARE, HO))
 
     def unit(b):
         quant("qe", "se", 128 * b, 128 * b + 128, v("ze", 3 - b, 515 - b))
 
     ts(pi(8), pi(0), 15, None, A.bitwise_and)
-    ts(pi(9), pi(0), 4, None, A.arith_shift_right)
-    ts(pi(10), pi(0), 4, 1, A.arith_shift_right, A.bitwise_and)
-    ts(pi(11), pi(0), 2, 3, A.arith_shift_right, A.bitwise_and)
-    ts(pi(12), pi(0), 3, None, A.bitwise_and)
-    cp(v("uo"), v("pi", 16, 24))
-    cp(v("cf", 0, 5), v("pi", 8, 13))
-    ms(v("ze"), 0.0)
+    ts(pi(9), pi(0), 4, 1, A.arith_shift_right, A.bitwise_and)
+    ts(pi(10), pi(0), 2, 3, A.arith_shift_right, A.bitwise_and)
+    ts(pi(11), pi(0), 3, None, A.bitwise_and)
+    cp(v("cf", 0, 4), v("pi", 8, 12))
     ts(v("hold"), v("m16"), cf(LANE), -BIG, A.is_le, A.mult)
     ts(v("kq"), v("m16"), 0.5, -2048.0, A.is_gt, A.mult)
-    quant("qu0", "su0", 0, 128, v("ub"))
-    ts(v("ze", 3, 515, 4), v("dif"), 0.0, None, A.is_equal)
-    cp(words(v("qu")), by(words(v("qu0")), v("uo")))
+    ts(v("pick16"), v("m16"), cf(LANE), None, A.is_equal)
+    for b in range(4):
+        unit(b)
     ts(v("kq", 0, C, 16), v("k0", 0, 25), cf(LANE), None, A.add)
-    unit(0)
+    cp(v("uo"), v("pi", 16, 24))
     ts(v("kq", 0, 1), cf(LANE), 16.0, None, A.add)
-    quant_x(0, HEAD)
-
-    plus(cf(LABL), cf(LANE), SLOT0 / 128.0, 1.0 / 128)
-    plus(cf(TH0), cf(LANE), 0.5 - STEP * SLOT0, -STEP)
-    plus(cf(TH1), cf(LANE), 0.5 - STEP * (SLOT0 + 1), -STEP)
-    plus(cf(LHALF), cf(LANE), 0.5)
-    plus(cf(KC), cf(LQ), 1.5, 2.0)
-    plus(v("pois"), v("hold"), -BIG, -2.0)
-    act(v("su"), by(v("su0"), v("uo")), F.Copy)
-    act(v("ab"), v("m16"), F.Abs, bias=cf(LANE), scale=-1.0)
-    act(v("keep16"), v("m16"), F.Sign)
-    act(v("pick16"), v("ab"), F.Relu, bias=1.0, scale=-1.0)
+    quant("qu0", "su0", 0, 128, v("ub"))
+    quant_x(0, 0, HEAD)
+    cp(words(v("qu")), by(words(v("qu0")), v("uo")))
 
     def keys(t):
-        plus(col(LGF), col(LG), cf(FARS + t))
-        plus(col(KEY2), col(CNT), col(LGF))
+        act(col(LGF), cf(LANE), F.Relu, bias=-(4.0 + t) * FAR, scale=FAR)
+        plus(col(KEY2), col(CNT), col(LG))
+        plus(col(KEY2), col(KEY2), col(LGF))
         plus(col(KEY1), col(KEY2), cf(LABL))
         plus(v("base", 32, 64), v("cross"), col(KEY2))
         plus(v("base", 0, 32), v("cross"), col(KEY1))
 
-    def late_constants():
-        act(cf(LG0), cf(LANE), F.Relu, bias=-0.625, scale=0.125)
-        plus(cf(PFAR), cf(PAR), 0.0, -FAR)
-        for t in range(R):
-            act(cf(FARS + t), cf(LANE), F.Relu, bias=-(4.0 + t) * FAR, scale=FAR)
-        plus(col(LG), cf(LANE), cf(LG0), 0.125)
-        act(v("cross"), v("d2"), F.Abs, bias=cf(PFAR), scale=FAR)
-        act(v("ab", 0, B), v("m4"), F.Abs, bias=cf(LQ), scale=-1.0)
-        keys(0)
-        act(v("pick4"), v("ab", 0, B), F.Relu, bias=1.0, scale=-1.0)
-        act(v("keep4"), v("m4"), F.Sign)
-        plus(v("kk"), v("k0", 0, 4), cf(LHALF))
+    plus(cf(GRP), cf(LANE), -7.5)
+    plus(cf(LABL), cf(LANE), SLOT0 / 128.0, 1.0 / 128)
+    if "s0" in PLAN:
+        plus(cf(TH0), cf(LANE), 0.5 - STEP * SLOT0, -STEP)
+        plus(cf(TH1), cf(LANE), 0.5 - STEP * (SLOT0 + 1), -STEP)
+    else:
+        plus(cf(MINE), cf(LANE), STEP * SLOT0, STEP)
+    for k in (2, 1, 3):
+        act(unwritten(k), v("m16", 0, 192), F.Copy, scale=0.0)
+    plus(v("pois"), v("hold"), -BIG, -2.0)
+    act(v("dg"), v("dif"), F.Abs, bias=cf(GRP))
+    plus(cf(LHALF), cf(LANE), 0.5)
+    act(v("dif"), v("dg"), F.Sign, bias=8.0, scale=-1.0)
+    act(v("su"), by(v("su0"), v("uo")), F.Copy)
+    for s in range(4):
+        act(v("zb", s, 512, 4), v("dif"), F.Relu)
+    act(cf(LG0), cf(LANE), F.Relu, bias=-0.625, scale=0.125)
+    plus(cf(PFAR), cf(PAR), 0.0, -FAR)
+    plus(v("kk"), v("k0", 0, 4), cf(LHALF))
+    plus(col(LG), cf(LANE), cf(LG0), 0.125)
 
-    def last_constants():
-        plus(v("own"), v("k0", 0, 16), cf(LANE))
-        plus(v("kc2"), v("k0", 0, 16), cf(KC), 0.5)
-        plus(v("dum"), v("own"), float(SPARE))
-        plus(cf(PAR16), cf(PAR), 0.0, 16.0)
-        for t in range(R):
-            plus(cf(LNEW + t), cf(PAR), 5.0 + t, 16.0)
-        plus(v("lc", 0, 25), v("lc", 32, 57), cf(PAR16))
+    def more_constants():
+        plus(v("pay"), v("pay0"), cf(TQ))
+        act(v("cross"), v("d2"), F.Abs, bias=cf(PFAR), scale=FAR)
+        act(v("ab"), v("m4"), F.Abs, bias=cf(LQ), scale=-1.0)
+        act(v("keep4"), v("m4"), F.Sign)
+        act(v("pick4"), v("ab"), F.Relu, bias=1.0, scale=-1.0)
+        plus(v("pad"), v("pad0"), cf(TQ))
+        keys(0)
 
     def slot(c, n0, n1):
         k, s = SLOT[c]
-        return v("tl%d" % k, 4 * n0 + s, 4 * n1, 4)
+        return v("tl", 4 * (TOFF[k] + n0) + s, 4 * (TOFF[k] + n1), 4)
 
     def score(c):
         return v("scn", 16 * c + 15, 16 * c + 16)
@@ -329,59 +342,66 @@ def rank_program(g, core, T, topo):
     def rsum(c):
         return v("rs", c, c + 1)
 
-    qoff = [sum(TW[:k]) for k in range(6)]
+    def tile_sum(ks, stop):
+        lo, hi = TOFF[ks[0]], TOFF[ks[-1]] + TW[ks[-1]]
+        quant("qc", "sc", lo, hi, v("tl", 4 * lo, 4 * hi))
+        for k in ks:
+            mx(2, QO, ("qc", "sc", TOFF[k], TOFF[k] + TW[k]), k == 0, stop and k == ks[-1])
 
-    def tile_sum(k, start, stop):
-        quant("qc", "sc", qoff[k], qoff[k] + TW[k], v("tl%d" % k))
-        mx(2, QO, ("qc", "sc", qoff[k], qoff[k] + TW[k]), start, stop)
-
-    def layer(bank0, x):
+    def layer(bank0, q, s, tile):
+        quant(q, s, 0, 128, v(tile))
         for b in range(4):
-            mx(bank0 + b, ("qw", "sw", 128 * b, 128 * b + 128), x)
+            mx(bank0 + b, ("qw", "sw", 128 * b, 128 * b + 128), (q, s, 0, 128))
 
-    def unpack(b):
-        mx(4 + b, ("qe", "se", 128 * b, 128 * b + 128), ("qx", "sx", 0, C))
+    def unpack(q, s, which):
+        for b in which:
+            mx(4 + b, ("qe", "se", 128 * b, 128 * b + 128), (q, s, 0, C))
 
-    q1, q2, r2 = v("er", 15, C, 16), v("rr", 0, 25), v("rr", 32, 57)
+    def copy_d(name, b):
+        act(v(name, b, 4 * C, 4), v("p%d" % (4 + b), 0, C), F.Copy)
 
-    def slots(t, step):
+    q1, q2, r2, rk = v("er", 15, C, 16), v("rr", 0, 25), v("rr", 32, 57), v("rk", 0, 25)
+    top = v("srt", 0, B)
+
+    def slots(step):
         if step == 0:
-            ts(v("lc", 32, 57), r2, B - 0.5, cf(LNEW + t), A.is_lt, A.mult)
+            ts(v("lc", 32, 57), r2, B - 0.5, cf(LNEW), A.is_lt, A.mult)
         else:
             tt(v("lc", 0, 25), v("lc", 0, 25), v("lc", 32, 57), A.max)
 
-    for t in range(R):
-        nk, ns = NK[t], NS[t]
+    def places(t):
+        qx, sx = "qx%d" % t, "sx%d" % t
 
-        mx(3, QU, ("qx", "sx", 0, HEAD))
-        quant_x(HEAD, C)
-        mx(0, QU, ("qx", "sx", 0, C))
-        mx(1, QU, ("qx", "sx", 0, 16 * max(ON_S)))
+        def rest():
+            quant_x(t, HEAD, C)
+            if EARLY:
+                send(raw(v("qr%d" % t)), raw(v(qx)), "arr%d" % t)
+                send(v("sr%d" % t), v(sx), "arr%d" % t)
+            mx(2, QU, (qx, sx, HEAD, C))
+            mx(0, QU, (qx, sx, 0, C))
+            mx(1, QU, (qx, sx, 0, 16 * max(ON_S)))
+
+        mx(3, QU, (qx, sx, 0, HEAD))
+        rest()
+        if t == 0:
+            late_fills()
         tt(v("rowp", 0, HEAD), v("p3", 0, HEAD), v("pois", 0, HEAD), A.min)
-        if t == 0:
-            unit(1)
-        else:
-            slots(t - 1, 0)
         scan(v("scn", 0, HEAD), v("hold", 0, HEAD), v("rowp", 0, HEAD), 0.0, A.add, A.max)
+        unpack(qx, sx, range(4))
+        tt(v("rowp", HEAD, C), v("p2", 0, C - HEAD), v("pois", HEAD, C), A.min)
         if t == 0:
-            unit(2)
-            unit(3)
-        else:
-            slots(t - 1, 1)
-        for b in range(4):
-            unpack(b)
-        tt(v("rowp", HEAD, C), v("p0", HEAD, C), v("pois", HEAD, C), A.min)
+            quant("qo", "so", 0, 128, v("zb"))
         scan(v("scn", HEAD, C), v("hold", HEAD, C), v("rowp", HEAD, C), 0.0, A.add, A.max)
 
         jobs = [(0, 16, 32), (1, 0, 16)] + [(c, 0, 16 * c) for c in ON_S]
 
         def sign(i):
             c, lo, hi = jobs[i]
-            act(v("sg%d" % (i % 3), 0, hi - lo), v("p3" if c < HEAD // 16 else "p1", lo, hi), F.Sign, bias=score(c), scale=-1.0)
+            act(v("sg%d" % (i % 4), 0, hi - lo), v("p3" if c < HEAD // 16 else "p1", lo, hi), F.Sign, bias=score(c), scale=-1.0)
 
         def positive(i):
             c, lo, hi = jobs[i]
-            sg = v("sg%d" % (i % 3), 0, hi - lo)
+            sg = v("sg%d" % (i % 4), 0, hi - lo)
             if c == 0:
                 act(v("ab", 0, 16), sg, F.Sign, bias=1.0, total=rsum(c))
             else:
@@ -393,143 +413,221 @@ def rank_program(g, core, T, topo):
                 sign(i + 1)
             positive(i)
         if t == 0:
-            plus(v("pay"), v("pay0"), cf(TQ))
+            more_constants()
         for b in range(4):
-            act(v("dx", b, 4 * C, 4), v("p%d" % (4 + b), 0, C), F.Copy)
-        if t == 0:
-            late_constants()
+            copy_d("dx", b)
 
         eo = slot("E", 0, C)
         tt(eo, v("scn"), v("p0", 0, C), A.is_ge)
-        if t == 0:
-            ts(v("zb"), v("dg"), cf(GRP), None, A.is_equal)
         tiles = [c for c in V_PLAN if isinstance(c, str) and c[0] == "q"]
         for c in V_PLAN:
             if c == "er":
                 scan(v("er"), v("kq"), eo, -2048.0, A.max, A.subtract)
             elif c in tiles:
-                if t == 0 and c == tiles[0]:
-                    quant("qo", "so", 0, 128, v("zb"))
-                tile_sum(int(c[1]), c == tiles[0], c == tiles[-1])
+                tile_sum([int(k) for k in c[1:]], c == tiles[-1])
             elif c > 0:
                 ts(slot(c, 0, 16 * c), v("p0", 0, 16 * c), score(c), None, A.is_lt)
             else:
                 e = 192 * (1 - c - V_LO)
                 scan(v("rh", e + 8 * c, e), slot(-c, 0, -8 * c), slot(-c, -8 * c, -16 * c), -128.0, A.add, A.add)
+        if EARLY:
+            landed([v("qr%d" % t), v("sr%d" % t)], "arr%d" % t, 2 * n_in)
         tt(q2, q1, v("rs", 0, 25), A.subtract)
-        tt(v("rr", V_LO, 25), v("rr", V_LO, 25), v("rh", 191, None, 192), A.subtract)
         tt(v("mm"), v("p2", 0, C), v("pick16"), A.mult)
-        scan(v("dd"), v("keep16"), v("mm"), 0.0, A.mult, A.add)
+        tt(v("rr", V_LO, 25), v("rr", V_LO, 25), v("rh", 191, 192 * (25 - V_LO), 192), A.subtract)
+        scan(v("dd"), v("keep16"), v("mm"), 0.0, A.min, A.add)
         tt(r2, v("dd", 15, C, 16), q2, A.add)
-        rk = v("rk", 0, 25)
         cp(rk, r2)
-
         cp(by(v("srt", 0, C), rk), v("pay"))
-        top = v("srt", 0, B)
-        act(v("sg0", 0, B), top, F.Sign, bias=cf(TH0), total=col(S0))
-        act(v("sg1", 0, B), top, F.Sign, bias=cf(TH1), total=col(S1))
-        plus(v("lab"), v("srt", B, C), -800.0 / FINE, 1.0 / FINE)
-        ts(v("lt"), top, -800.0, None, A.add)
-        tt(g80, top, v("lt"), A.subtract)
-        ts(v("kr"), v("base"), col(S0), col(S1), A.subtract, A.add)
-        turn(v("kt"), v("kr"))
-        red(col(VM2), v("kt", 32, 64), A.min)
-        red(col(VM1), v("kt", 0, 32), A.min)
-        cs, cl = v("cs%d" % t, 0, 1), v("cl%d" % t, 0, 1)
-        plus(cs, col(VM2), 0.0, -FINE)
-        send(cl, cs, "cnt%d" % t)
-        plus(col(VV), col(VM1), cs, FINE)
 
-        ts(v("ind"), v("lab"), col(VM2), col(VM1), A.add, A.is_equal)
-        scan(v("cnt"), v("ind"), v("ind"), 0.0, A.add, A.max)
-        for k in range(1, nk):
-            act(v("sg%d" % (k % 2), 0, 304), v("cnt", 16, 320), F.Sign, bias=v("kk", k, k + 1), scale=-1.0,
-                total=v("pb", 160 * k + 159, 160 * k + 160))
-        ts(v("le"), v("cnt"), v("kk", 0, 1), 2.0, A.is_lt, A.mult)
-        tt(h80, g80, v("pick4"), A.mult)
-        scan(v("pb", 0, 160), v("le", 0, 160), v("le", 160, 320), -336.0, A.add, A.add)
-        scan(i80, v("keep4"), h80, 0.0, A.mult, A.add)
+    def behind(t):
+        nk, nv, cut, last = NK[t], KN["nv"][t], KN["cut"], t + 1 == R
+        n4, w, lo = 4 * nk, 16 * nk, 16 * nv
+        gl, gr, off, xs = v("gl%d" % t, 0, n4), v("gr%d" % t, 0, n4), v("off", 0, n4), v("xs", 3, w, 4)
+        hm = [v("hm", 16 * k, 16 * k + n4) for k in range(3)]
+
+        def search_s():
+            for k in range(nv, nk):
+                act(v("sg%d" % (k % 2), lo, 320 + w), v("cnt", lo, 320 + w), F.Sign, bias=v("kk", k, k + 1), scale=-1.0,
+                    total=v("pb", 168 * k + 167, 168 * k + 168))
+
+        def below():
+            for k in range(nv):
+                ts(v("le", 336 * k, 336 * k + 336), v("cnt", 16 * k, 16 * k + 336), v("kk", k, k + 1), 2.0, A.is_lt, A.mult)
+
+        def search_v():
+            for k in range(nv):
+                scan(v("pb", 168 * k, 168 * k + 168), v("le", 336 * k, 336 * k + 168), v("le", 336 * k + 168, 336 * k + 336),
+                     32.0 * k - 320.0 - w - lo, A.add, A.add)
+
+        def send_list():
+            ts(gl, xs, col(VV), None, A.subtract)
+            send(gr, gl, "lst%d" % t)
+            landed([gr], "lst%d" % t, n_in)
+
+        def shared(out, win, lst, on_v):
+            if on_v < n4:
+                act(v(out, 16 * on_v, 4 * w), by(v(win), v(lst, on_v, n4)), F.Copy)
+            if on_v:
+                cp(v(out, 0, 16 * on_v), by(v(win), v(lst, 0, on_v)))
+
+        def scaled(name, first, n, bank0):
+            for b in range(4):
+                act(v(name, first + b, first + 4 * n, 4), v("p%d" % (bank0 + b), 0, n), F.Copy, scale=0.03125)
+
+        due, due_t = list(range(4)), list(range(4))
+        qt, sq, ns = "qr%d" % t, "sr%d" % t, NS[t]
+        cs, cl = (None, None) if EARLY else (v("cs%d" % t, 0, 1), v("cl%d" % t, 0, 1))
+
+        def send_count():
+            plus(cs, col(VM2), 0.0, -FINE)
+            send(cl, cs, "lst%d" % t)
+            landed([cl], "lst%d" % t, n_in)
+
+        def send_s():
+            qs, ss = "qs%d" % t, "ss%d" % t
+            quant(qs, ss, 0, 128, v("sb"))
+            send(raw(v(qt, 128, 128 + ns)), raw(v(qs, 0, ns)), "arr%d" % t)
+            send(v(sq, 128, 128 + ns), v(ss, 0, ns), "arr%d" % t)
+            landed([v(qt, 128, 128 + ns), v(sq, 128, 128 + ns)], "arr%d" % t, 2 * n_in)
+
+        def h2():
+            for b in range(4):
+                mx(4 + b, ("qw", "sw", 128 * b, 128 * b + 128), (qt, sq, ns, 128 + ns))
+            for b in range(4):
+                act(v("sb", 256 + b, 256 + 4 * ns, 4), v("p%d" % (4 + b), 128 - ns, 128), F.Copy, scale=0.03125)
+
+        def put_y(a, b):
+            if a < b:
+                cp(by(v("st"), v("to", a, b)), v("yt", 16 * a, 16 * b))
 
         def relabel():
-            ts(col(CNT), col(CNT), col(S0), col(S1), A.subtract, A.add)
-            ts(col(ISV), col(CNT), col(LGF), col(VM2), A.add, A.is_equal)
-            ts(col(LG), col(ISV), (6 + 2 * t) / 8.0, col(LG), A.mult, A.max)
+            plus(col(VF), col(VM2), 0.0, -FINE)
+            plus(col(KEY1), col(KEY2), col(W2))
+            plus(col(LGF), col(LG), (6 + 2 * t) / 8.0, -1.0)
+            act(col(KEY1), col(KEY1), F.Abs, bias=col(VF), scale=FINE)
+            plus(col(CNT), col(CNT), col(W2))
+            act(col(ISV), col(KEY1), F.Relu, bias=1.0, scale=-1.0)
+            act(col(LG), col(ISV), F.Identity, bias=col(LG), scale=col(LGF))
 
-        cp(v("to"), v("w80", 2 * B + 3, 3 * B, 4))
-        act(v("tt", 0, 4 * B), by(pages(0, C), v("to")), F.Copy)
-        if nk == 4:
-            relabel()
-        w = 16 * nk
-        ts(v("pos", 0, nk), v("pb", 159, 160 * nk, 160), 0.5, 248.0, A.mult, A.add)
-        tt(v("xg", 0, w), by(v("srt"), v("pos", 0, nk)), v("pick4", 0, w), A.mult)
-        scan(v("xs", 0, w), v("keep4", 0, w), v("xg", 0, w), 0.0, A.mult, A.add)
-        xs = v("xs", 3, w, 4)
-        ts(v("gl", 0, 4 * nk), xs, col(VV), float(SPARE), A.subtract, A.min)
+        def late():
+            if t == 0:
+                if EARLY:
+                    plus(v("dum"), v("own"), cf(LANE))
+                else:
+                    plus(v("dum"), v("k0", 0, 16), cf(LANE))
+                    plus(cf(LNEW), cf(LQ), 1.5, 2.0)
+                    plus(v("kc2"), v("k0", 0, 16), cf(LNEW), 0.5)
+                plus(cf(PAR16), cf(PAR), 0.0, 16.0)
+                plus(v("lc", 0, 25), v("lc", 32, 57), cf(PAR16))
+            plus(cf(LNEW), cf(PAR), 5.0 + t, 16.0)
 
-        act(v("sb", 2 * w, 4 * w), by(v("dx"), v("gl", 2 * nk, 4 * nk)), F.Copy)
-        cp(v("sb", 0, 2 * w), by(v("dx"), v("gl", 0, 2 * nk)))
-        qs, ss, qt, sq = "qs%d" % t, "ss%d" % t, "qt%d" % t, "sq%d" % t
-        quant(qs, ss, 0, 128, v("sb"))
-        send(raw(v(qt, 128, 128 + ns)), raw(v(qs, 0, ns)), "arr%d" % t)
-        send(v(sq, 128, 128 + ns), v(ss, 0, ns), "arr%d" % t)
+        def ends():
+            if last:
+                quant("qv", "sv", 0, 128, v("vb"))
+                cp(v("lu", 0, 25), v("lc", 0, 25))
 
-        quant(qt, sq, 0, 128, v("tt"))
-        layer(0, (qt, sq, 0, 128))
-        if t == 0:
-            last_constants()
-        off = v("off", 0, 4 * nk)
-        ts(off, xs, col(VV), None, A.subtract)
-        if nk < 4:
-            relabel()
-        tt(v("slf", 0, 4 * nk), off, v("dum", 0, 4 * nk), A.min)
-        cp(v("sl", 0, 4 * nk), v("slf", 0, 4 * nk))
-        landed([cl], "cnt%d" % t, n_in)
-        hm = [v("hm", 16 * k, 16 * k + 4 * nk) for k in range(3)]
-        act(hm[0], v("kc2", 0, 4 * nk), F.Sign, bias=cl, scale=FINE)
-        if t + 1 < R:
-            plus(top, g80, STEP * (SLOT0 + 5 + t))
-        plus(hm[1], hm[0], 128.0, -128.0)
-        for b in range(4):
-            act(v("yt", b, 4 * B, 4), v("p%d" % b, 0, B), F.Copy, scale=0.03125)
-        tt(hm[2], hm[1], v("own", 0, 4 * nk), A.add)
-        if t + 1 == R:
-            slots(t, 0)
-            quant("qv", "sv", 0, 128, v("vb"))
-            slots(t, 1)
-        cp(v("hl", 0, 4 * nk), hm[2])
-        if t + 1 < R:
-            act(v("pay"), by(v("srt", 0, C), rk), F.Copy)
+        def new_top():
+            if last:
+                relabel()
+                plus(v("tb", 0, 32), v("cross"), col(LG), 0.0)
+            else:
+                plus(top, g80, STEP * (SLOT0 + 5 + t))
+
+        def following():
+            if last:
+                act(v("lf"), by(v("tb", 32, 64), v("lu", 0, 25)), F.Copy, scale=8.0)
+                store("a", T.ob[:], (T.lf[0:128:16, :], v("lf")[1]))
+            else:
+                quant_x(t + 1, 0, HEAD)
+                relabel()
+                keys(t + 1)
+
+        steps = {
+            "lab": lambda: plus(v("lab"), v("srt", B, C), -800.0 / FINE, 1.0 / FINE),
+            "lt": lambda: ts(v("lt"), top, -800.0, None, A.add),
+            "eq": lambda: ts(v("le", 0, B), v("lt"), cf(MINE), -2.0, A.is_equal, A.mult),
+            "written": lambda: red(col(W2), v("le", 0, B), A.add),
+            "kr": lambda: ts(v("kr"), v("base"), col(W2), None, A.add),
+            "turn": lambda: turn(v("kt"), v("kr")),
+            "vm2": lambda: red(col(VM2), v("kt", 32, 64), A.min),
+            "vm1": lambda: red(col(VM1), v("kt", 0, 32), A.min),
+            "vv": lambda: ts(col(VV), col(VM1), col(VM2), FINE, A.subtract, A.mult),
+            "pad": lambda: plus(v("srt", C, C + w), v("pad", 0, w), col(VV)),
+            "ind": lambda: ts(v("ind", 0, 320), v("lab"), col(VM2), col(VM1), A.add, A.is_equal),
+            "cnt": lambda: scan(v("cnt", 0, 320 + w), v("ind", 0, 320 + w), v("ind", 0, 320 + w), 0.0, A.add, A.max),
+            "search_s": search_s, "below": below, "search_v": search_v,
+            "pos": lambda: ts(v("pos", 0, nk), v("pb", 167, 168 * nk, 168), 0.5, 240.0 + (w + lo) / 2, A.mult, A.add),
+            "xg": lambda: tt(v("xg", 0, w), by(v("srt", 0, C + w), v("pos", 0, nk)), v("pick4", 0, w), A.mult),
+            "xs": lambda: scan(v("xs", 0, w), v("keep4", 0, w), v("xg", 0, w), 0.0, A.mult, A.add),
+            "gl": send_list,
+            "g80": lambda: tt(g80, top, v("lt"), A.subtract),
+            "h80": lambda: tt(h80, g80, v("pick4"), A.mult),
+            "i80": lambda: scan(i80, v("keep4"), h80, 0.0, A.mult, A.add),
+            "to": lambda: cp(v("to"), v("w80", 2 * B + 3, 3 * B, 4)),
+            "take_t": lambda: act(v("tt", 0, 4 * B), by(pages(0, C), v("to")), F.Copy),
+            "quant_t": lambda: layer(0, "qt", "sq", "tt"),
+            "y": lambda: scaled("yt", 0, B, 0),
+            "put_y": lambda: put_y(0, cut), "rest_y": lambda: put_y(cut, 20),
+            "u": lambda: unpack("qr%d" % t, "sr%d" % t, [due_t.pop(0)]), "d": lambda: due and copy_d("dy", due.pop(0)),
+            "e": lambda: t > 0 and copy_d("dy", due.pop(0)),
+            "dv": lambda: due and cp(v("dy", due[0], 4 * C, 4), v("p%d" % (4 + due.pop(0)), 0, C)),
+            "s0": lambda: act(v("sg0", 0, B), top, F.Sign, bias=cf(TH0), total=col(S0)),
+            "s1": lambda: act(v("sg1", 0, B), top, F.Sign, bias=cf(TH1), total=col(S1)),
+            "kr2": lambda: ts(v("kr"), v("base"), col(S0), col(S1), A.subtract, A.add),
+            "w2": lambda: plus(col(W2), col(S0), col(S1), -1.0),
+            "krs": lambda: plus(v("kr"), v("base"), col(W2)),
+            "slot0": lambda: slots(0), "slot1": lambda: slots(1),
+            "off": lambda: plus(off, v("dum", 0, n4), col(VV)),
+            "top": new_top, "pay": lambda: last or act(v("pay"), by(v("srt", 0, C), rk), F.Copy),
+            "take_s": lambda: shared("sb", "dy", "gr%d" % t, KN["sv"] * 2 * nk),
+            "quant_s": lambda: layer(4, "qs", "ss", "sb"),
+            "hm0": lambda: ts(hm[0], gr, SPARE - 0.5, 1e6, A.is_lt, A.mult),
+            "hm1": lambda: tt(hm[1], hm[0], off, A.min),
+            "hm2": lambda: tt(hm[2], hm[1], xs, A.max),
+            "hl": lambda: ts(v("hl", 0, n4), hm[2], col(VV), None, A.subtract),
+            "h": lambda: scaled("dx", HO, w, 4),
+            "take_z": lambda: shared("zt", "dx", "hl", KN["zv"] * 2 * nk),
+            "put_z": lambda: cp(by(v("st"), gl), v("zt", 0, 4 * w)),
+            "labels": lambda: last and turn(v("tb", 32, 64), v("tb", 0, 32)),
+            "cs": send_count, "vv2": lambda: plus(col(VV), col(VM1), cs, FINE),
+            "gl2": lambda: ts(gl, xs, col(VV), None, A.subtract),
+            "take_s2": lambda: shared("sb", "dx", "gl%d" % t, KN["sv"] * 2 * nk),
+            "send_s": send_s,
+            "quant_t2": lambda: layer(0, qt, sq, "tt"),
+            "hs0": lambda: act(hm[0], v("kc2", 0, n4), F.Sign, bias=cl, scale=FINE),
+            "hs1": lambda: plus(hm[1], hm[0], 128.0, -128.0),
+            "hs2": lambda: tt(hm[2], hm[1], v("dum", 0, n4), A.add),
+            "hs3": lambda: cp(v("hl", 0, n4), hm[2]),
+            "h2": h2,
+            "take_z2": lambda: shared("zt", "sb", "hl", KN["zv"] * 2 * nk),
+            "late": late, "ends": ends, "next": following}
+        done = set()
+        for name in PLAN:
+            if name[-1] == "'":
+                if t > 0:
+                    done.add(name[:-1])
+                    steps[name[:-1]]()
+            elif name not in done:
+                steps[name]()
+
+    for t in range(R):
+        places(t)
+        behind(t)
+
+    qx, sx = "qx%d" % R, "sx%d" % R
+    for k, (lo, hi) in enumerate(PIECES):
+        quant_x(R, lo, hi)
+        mx(k, QV, (qx, sx, lo, hi))
+    for k, (lo, hi) in enumerate(PIECES):
+        store("s", T.oc[:, 4 * lo:4 * hi], raw(v(qx, lo, hi)))
+        if k > 0:
+            cp(v("yb", lo, hi), v("p%d" % k, 0, hi - lo))
         else:
-            plus(v("tb", 0, 32), v("cross"), col(LG), 0.0)
-            cp(v("lu", 0, 25), v("lc", 0, 25))
-            turn(v("tb", 32, 64), v("tb", 0, 32))
-            act(v("lf"), by(v("tb", 32, 64), v("lu", 0, 25)), F.Copy, scale=8.0)
-            store("a", T.ob[:], (T.lf[0:128:16, :], v("lf")[1]))
-        cp(by(v("st"), v("to")), v("yt"))
-
-        landed([v(qt, 128, 128 + ns), v(sq, 128, 128 + ns)], "arr%d" % t, 2 * n_in)
-        layer(4, (qt, sq, ns, 128 + ns))
-        for b in range(4):
-            act(v("sb", 256 + b, 256 + 4 * ns, 4), v("p%d" % (4 + b), 128 - ns, 128), F.Copy, scale=0.03125)
-        act(v("zt", 2 * w, 4 * w), by(v("sb"), v("hl", 2 * nk, 4 * nk)), F.Copy)
-        cp(v("zt", 0, 2 * w), by(v("sb"), v("hl", 0, 2 * nk)))
-        cp(by(v("st"), v("sl", 0, 4 * nk)), v("zt", 0, 4 * w))
-        if t + 1 < R:
-            keys(t + 1)
-            quant_x(0, HEAD)
-
-    quant_x(0, TAIL)
-    mx(0, QV, ("qx", "sx", 0, TAIL))
-    store("s", T.oc[:, 0:4 * TAIL], raw(v("qx", 0, TAIL)))
-    quant_x(TAIL, C)
-    mx(1, QV, ("qx", "sx", TAIL, C))
-    act(v("yb", 0, TAIL), v("p0", 0, TAIL), F.Copy)
-    cp(v("yb", TAIL, C), v("p1", 0, C - TAIL))
-    store("s", T.oc[:, 4 * TAIL:4 * C], raw(v("qx", TAIL, C)))
-    store("a", T.y[:, 0:TAIL], v("yb", 0, TAIL))
+            act(v("yb", lo, hi), v("p%d" % k, 0, hi - lo), F.Copy)
+        store("a", T.y[:, lo:hi], v("yb", lo, hi))
     for k in range(4):
-        store("s", T.osc[4 * k:4 * k + 4, :], (T.sx[32 * k:32 * k + 4, :], v("sx")[1]))
-    store("a", T.y[:, TAIL:C], v("yb", TAIL, C))
+        store("s", T.osc[4 * k:4 * k + 4, :], (T[sx][32 * k:32 * k + 4, :], v(sx)[1]))
     for sem in SEMAPHORES:
         if sem in count:
             g.wait_ge(T.sem[sem], count[sem])

from concourse.mybir import dt, AluOpType as A, AxisListType, ActivationFunctionType as F

C, B, R = 400, 80, 3
NK = (4, 4, 3)
NS = (64, 56, 48)
BIG = 1e29
FAR = 8192.0
SPARE = 4 * C
HO = SPARE + 256
HEAD = 128
PIECES = ((0, 136), (136, 272), (272, C))
TW = (400, 336, 272, 208, 144, 128)
SLOT = {"E": (0, 0)}
for _c in range(24, 1, -1):
    SLOT[_c] = ((25 - _c) // 4, (25 - _c) % 4)
TILES = (0, 1, 5, 2, 3, 4)
TOFF = {_k: sum(TW[_j] for _j in TILES[:TILES.index(_k)]) for _k in TILES}
ON_S = (5, 4, 3, 2, 7, 6, 16, 15, 14, 13, 12, 11, 10, 9, 8)
V_LO = 17
V_PLAN = (24, 23, 22, 21, "q0", 20, 19, 18, 17, "q15", "er", "q2", -24, -23, -22, "q3", -21, -20, "q4", -19, -18, -17)
PLAN = ("u u u u e e e s0 s1 lab lt g80 kr2 h80 turn i80 vm2 vm1 to take_t ind vv cnt pad search_s below quant_t search_v pos d late "
        "xg xs gl y d d d off w2' top' pay' slot0 put_y slot1 ends take_s w2 top hm0 quant_s hm1 pay hm2 hl rest_y labels h take_z put_z "
        "next").split()
KN = {"nv": (2, 2, 2), "cut": 12, "sv": 1, "zv": 1}
STEP = 2048.0
SLOT0 = 129
FINE = 128.0 * STEP

Q8, U8, BF, F16, F32, I32, U16 = "float8_e4m3fn_x4", "uint8", "bfloat16", "float16", "float32", "int32", "uint16"
SCRATCH = {}


def _sb(name, n, d):
    SCRATCH[name] = ("sbuf", [128, n], d)


for _k in range(8):
    SCRATCH["p%d" % _k] = ("psum", [128, 512], F32)
for _t in range(R):
    _sb("qr%d" % _t, C, Q8); _sb("sr%d" % _t, C, U8)
    _sb("gl%d" % _t, 16, U16); _sb("gr%d" % _t, 16, U16)
    if "u" not in PLAN:
        _sb("qs%d" % _t, 128, Q8); _sb("ss%d" % _t, 128, U8)
        _sb("cs%d" % _t, 4, F32); _sb("cl%d" % _t, 4, F32)
for _t in range(R + 1):
    _sb("qx%d" % _t, C, Q8); _sb("sx%d" % _t, C, U8)
for _n, _w, _d in (
        ("tl", 4 * sum(TW), BF), ("sg3", 384, BF),
        ("st", SPARE + 256, BF), ("dx", HO + 256, BF), ("dy", HO, BF), ("qc", 1488, Q8), ("sc", 1488, U8),
        ("qs", 128, Q8), ("ss", 128, U8), ("qt", 128, Q8), ("sq", 128, U8),
        ("ub", 512, BF), ("vb", 512, BF), ("qu0", 128, Q8), ("su0", 128, U8), ("qu", 128, Q8), ("su", 128, U8),
        ("qv", 128, Q8), ("sv", 128, U8), ("qw", 512, Q8), ("sw", 512, U8),
        ("qe", 512, Q8), ("se", 512, U8), ("qo", 128, Q8), ("so", 128, U8),
        ("ze", 520, BF), ("zb", 512, BF), ("tt", 512, BF), ("sb", 512, BF), ("yt", 320, BF), ("zt", 256, BF),
        ("pi", 24, I32), ("cf", 16, F32), ("uo", 8, U16),
        ("dif", 128, BF), ("dg", 128, BF), ("d2", 32, F32), ("m16", C, BF), ("m4", B, BF), ("ab", B, BF),
        ("hold", C, BF), ("pois", C, BF), ("pick16", C, BF), ("keep16", C, BF), ("kq", C, F16), ("pick4", B, BF), ("keep4", B, BF),
        ("cross", 32, F32), ("k0", 32, F32), ("kk", 4, F32), ("own", 16, F32), ("kc2", 16, F32), ("dum", 16, F32), ("pay0", C, F32),
        ("rowp", C, F32), ("scn", C, F32), ("sg0", 384, BF), ("sg1", 384, BF), ("sg2", 384, BF),
        ("rs", 32, F32), ("rh", 192 * 12, BF), ("er", C, F16), ("rr", 96, F32), ("mm", C, F16), ("dd", C, F16),
        ("rk", 26, U16), ("pay", C, F32), ("srt", C + 64, F32),
        ("lt", B, BF), ("base", 64, F32), ("lab", 320, BF), ("col", 16, F32), ("kr", 64, F32), ("kt", 64, F32),
        ("ind", 384, BF), ("cnt", 384, BF), ("le", 1344, BF), ("pb", 672, F32), ("pad0", 64, F32), ("pad", 64, F32),
        ("pos", 4, U16), ("xg", 64, F32), ("xs", 64, F32), ("off", 16, F32),
        ("hm", 48, F32), ("hl", 16, U16), ("w80", 240, F32), ("to", 20, U16),
        ("lc", 64, F32), ("lu", 26, U16), ("tb", 64, F32), ("yb", C, F32), ("lf", C, F32)):
    _sb(_n, _w, _d)

SEMAPHORES = (["cv", "ca", "ct", "cg", "ldu", "ldx", "ldy", "ldw", "lds", "ldv", "out", "loc"]
              + ["lst%d" % _t for _t in range(R)] + ["arr%d" % _t for _t in range(R)])

LANE, PAR, LQ, TQ, GRP, LABL, MINE, LHALF, LG0, PFAR, PAR16, LNEW, TH0, TH1 = range(14)
W2, VF, VM1, VM2, VV, CNT, ISV, LG, LGF, KEY2, KEY1, S0, S1 = range(13)


def rank_program(g, core, T, topo):
    EARLY = "u" in PLAN
    rank = T.rank_of(core)
    if rank is None:
        return
    n_ranks = len(T.cores)
    nxt, prv = T.cores[(rank + 1) % n_ranks], T.cores[(rank - 1) % n_ranks]
    rid, pid = topo.addr(nxt, core)
    mask_out = topo.mask(core, nxt)
    n_out, n_in = len(topo.engines(core, nxt)), len(topo.engines(prv, core))

    def v(name, lo=0, hi=None, step=1):
        hi = SCRATCH[name][1][1] if hi is None else hi
        ap = T[name][:, lo:hi] if step == 1 else T[name][:, lo:hi:step]
        return ap, [(name, range(0, 1) if SCRATCH[name][0] == "psum" else range(lo, hi, step))]

    def words(x):
        return x[0].bitcast(dt.uint32), x[1]

    def raw(x):
        return x[0].bitcast(dt.uint8), x[1]

    def by(x, off):
        return x[0].indirect(off[0]), x[1], off[1]

    def ap(x):
        return x[0] if isinstance(x, tuple) else x

    eng = {"v": g.vector, "a": g.scalar, "t": g.tensor, "g": g, "s": g.sync}
    own = {"v": "cv", "a": "ca", "t": "ct", "g": "cg"}
    count, seen = {}, {e: {} for e in eng}
    wrote = {n: {} for n in SCRATCH}
    read = {n: {} for n in SCRATCH}

    def wait(e, tok):
        sem, val, clock, _ = tok
        if seen[e].get(sem, 0) < val:
            eng[e].wait_ge(T.sem[sem], val)
            seen[e][sem] = val
        for s, n in clock.items():
            if seen[e].get(s, 0) < n:
                seen[e][s] = n

    def order(e, rd, wr, acc):
        need = {}

        def add(tok):
            if tok[1] > need.get(tok[0], (0, 0))[1]:
                need[tok[0]] = tok

        for name, cols in rd:
            for c in cols:
                if c in wrote[name]:
                    add(wrote[name][c])
            if SCRATCH[name][0] == "psum":
                for x in read[name].get(0, {}).values():
                    if x[3] != e:
                        add(x)
        for name, cols in wr:
            for c in cols:
                if c in wrote[name] and not (acc and wrote[name][c][3] == e):
                    add(wrote[name][c])
                for x in read[name].get(c, {}).values():
                    add(x)
        for tok in sorted(need.values(), key=lambda x: -len(x[2])):
            wait(e, tok)

    def note(tok, rd, wr):
        for name, cols in rd:
            for c in cols:
                read[name].setdefault(c, {})[tok[0]] = tok
        for name, cols in wr:
            for c in cols:
                wrote[name][c] = tok
                read[name][c] = {}

    def op(e, call, ins, outs, acc=False, sem=None, inc=1):
        rd = [r for x in ins if isinstance(x, tuple) for part in x[1:] for r in part] + [r for x in outs for part in x[2:] for r in part]
        wr = [r for x in outs for r in x[1]]
        order(e, rd, wr, acc)
        sem = sem or own[e]
        call().then_inc(T.sem[sem], inc)
        count[sem] = count.get(sem, 0) + inc
        note((sem, count[sem], dict(seen[e]), e), rd, wr)

    def load(e, out, src, sem, after=()):
        op(e, lambda: eng[e].dma_start(out[0], src), list(after), [out], sem=sem, inc=16)

    def store(e, dst, in_):
        op(e, lambda: eng[e].dma_start(dst, in_[0]), [in_], [], sem="out", inc=16)

    def ts(out, in0, s1, s2, o0, o1=None):
        if s2 is None:
            return op("v", lambda: g.vector.tensor_scalar(out[0], in0[0], ap(s1), None, o0), [in0, s1], [out])
        return op("v", lambda: g.vector.tensor_scalar(out[0], in0[0], ap(s1), ap(s2), o0, o1), [in0, s1, s2], [out])

    def tt(out, in0, in1, o):
        op("v", lambda: g.vector.tensor_tensor(out[0], in0[0], in1[0], o), [in0, in1], [out])

    def cp(out, in_):
        op("v", lambda: g.vector.tensor_copy(out[0], in_[0]), [in_], [out])

    def ms(out, val):
        op("v", lambda: g.vector.memset(out[0], val), [], [out])

    def scan(out, d0, d1, init, o0, o1):
        op("v", lambda: g.vector.tensor_tensor_scan(out[0], d0[0], d1[0], init, o0, o1), [d0, d1], [out])

    def red(out, in_, o):
        op("v", lambda: g.vector.tensor_reduce(out[0], in_[0], AxisListType.X, o), [in_], [out])

    def turn(out, in_):
        op("v", lambda: g.vector.transpose(out[0], in_[0]), [in_], [out])

    def quant(q, s, lo, hi, in_):
        qq, ss = v(q, lo, hi), v(s, lo, hi)
        op("v", lambda: g.vector.quantize_mx(qq[0], ss[0], in_[0]), [in_], [qq, ss])

    def act(out, in_, f, bias=None, scale=None, total=None):
        kw = {k: ap(x) for k, x in (("bias", bias), ("scale", scale), ("accum_out", total)) if x is not None}
        op("a", lambda: g.scalar.activation(out[0], in_[0], f, **kw), [in_, bias, scale], [out] + ([total] if total else []))

    def plus(out, in_, b, scale=1.0):
        act(out, in_, F.Identity, bias=b, scale=scale)

    def mx(bank, w, x, start=True, stop=True):
        a = [v(w[0], w[2], w[3]), v(w[1], w[2], w[3]), v(x[0], x[2], x[3]), v(x[1], x[2], x[3])]
        out = v("p%d" % bank, 0, x[3] - x[2])
        op("t", lambda: g.tensor.matmul_mx(out[0], a[0][0], a[1][0], a[2][0], a[3][0], start, stop), a, [out], acc=not start)

    def iota(out, pat, base, cm, whole=False):
        if whole:
            return op("g", lambda: g.iota(out[0], pat, base, cm), [], [out])
        return op("g", lambda: g.iota(out[0], pat, base, cm, allow_small_or_imprecise_dtypes=True), [], [out])

    def fill(out, val=0):
        iota(out, [[0, len(out[1][0][1])]], val, 0)

    def send(out, in_, sem):
        order("g", in_[1], [], False)
        g.remote_dma(out[0], in_[0], T.sem[sem], T.sem.loc, pid, rid, mask_out)
        count["loc"] = count.get("loc", 0) + n_out

    def landed(views, sem, n):
        note((sem, n, {}, "r"), [], [r for x in views for r in x[1]])

    def cf(k):
        return v("cf", k, k + 1)

    def col(k):
        return v("col", k, k + 1)

    def pi(k):
        return v("pi", k, k + 1)

    def pages(lo, hi):
        return v("st", 4 * lo, 4 * hi)

    def quant_x(t, lo, hi):
        quant("qx%d" % t, "sx%d" % t, lo, hi, pages(lo, hi))

    QU, QV, QO = ("qu", "su", 0, 128), ("qv", "sv", 0, 128), ("qo", "so", 0, 128)
    g80, h80, i80 = [v("w80", B * k, B * k + B) for k in range(3)]

    load("a", v("ub"), T.u[:], "ldu")
    load("s", pages(0, HEAD), T.x[:, 0:4 * HEAD], "ldx")
    load("s", pages(HEAD, C), T.x[:, 4 * HEAD:4 * C], "ldy")
    load("s", raw(v("qw")), T.wc[:], "ldw", [pages(HEAD, C)])
    load("s", v("sw"), T.ws[:], "lds")
    load("s", v("vb"), T.v[:], "ldv")

    def unwritten(k):
        return v("tl", 4 * TOFF[k] + 64 * min(c for c in range(2, 25) if SLOT[c][0] == k), 4 * (TOFF[k] + TW[k]))

    ms(v("ze"), 0.0)
    iota(pi(0), [[0, 1]], 0, 1, True)
    iota(v("m16"), [[0, 25], [1, 16]], 0, 0)
    one = v("ze", 3, 515, 4)
    op("g", lambda: g.affine_select(one[0], one[0], [[1, 128]], A.not_equal, 1.0, 0, -1), [one], [one])
    iota(v("k0", 0, 25), [[16, 25]], 0, 0)
    iota(v("pi", 16, 24), [[16, 8]], 0, 0, True)
    iota(v("dif"), [[1, 128]], 0, -1)
    for k in (5, 0, 4):
        fill(unwritten(k))
    iota(v("d2"), [[1, 2], [0, 16]], 0, 0)
    fill(col(CNT), 2 * B)
    iota(v("m4"), [[0, 20], [1, 4]], 0, 0)
    iota(v("pay0"), [[int(STEP) + 4 * B, 5], [4, B]], int(STEP) * SLOT0, 0)
    fill(v("rs", V_LO, 25), 128)
    iota(v("pad0"), [[4, 64]], SPARE, 0)
    fill(v("ind", 320), 1)

    def late_fills():
        iota(v("keep16"), [[0, 25], [2048, 16]], 0, 0)
        fill(v("tt", 4 * B))
        iota(v("own"), [[16, 16]], HO, 0)
        iota(v("lc", 32, 57), [[1, 5], [0, 5]], 0, 0)
        fill(v("dy", SPARE))
        fill(v("sb", 256))
        fill(v("dx", SPARE, HO))

    def unit(b):
        quant("qe", "se", 128 * b, 128 * b + 128, v("ze", 3 - b, 515 - b))

    ts(pi(8), pi(0), 15, None, A.bitwise_and)
    ts(pi(9), pi(0), 4, 1, A.arith_shift_right, A.bitwise_and)
    ts(pi(10), pi(0), 2, 3, A.arith_shift_right, A.bitwise_and)
    ts(pi(11), pi(0), 3, None, A.bitwise_and)
    cp(v("cf", 0, 4), v("pi", 8, 12))
    ts(v("hold"), v("m16"), cf(LANE), -BIG, A.is_le, A.mult)
    ts(v("kq"), v("m16"), 0.5, -2048.0, A.is_gt, A.mult)
    ts(v("pick16"), v("m16"), cf(LANE), None, A.is_equal)
    for b in range(4):
        unit(b)
    ts(v("kq", 0, C, 16), v("k0", 0, 25), cf(LANE), None, A.add)
    cp(v("uo"), v("pi", 16, 24))
    ts(v("kq", 0, 1), cf(LANE), 16.0, None, A.add)
    quant("qu0", "su0", 0, 128, v("ub"))
    quant_x(0, 0, HEAD)
    cp(words(v("qu")), by(words(v("qu0")), v("uo")))

    def keys(t):
        act(col(LGF), cf(LANE), F.Relu, bias=-(4.0 + t) * FAR, scale=FAR)
        plus(col(KEY2), col(CNT), col(LG))
        plus(col(KEY2), col(KEY2), col(LGF))
        plus(col(KEY1), col(KEY2), cf(LABL))
        plus(v("base", 32, 64), v("cross"), col(KEY2))
        plus(v("base", 0, 32), v("cross"), col(KEY1))

    plus(cf(GRP), cf(LANE), -7.5)
    plus(cf(LABL), cf(LANE), SLOT0 / 128.0, 1.0 / 128)
    if "s0" in PLAN:
        plus(cf(TH0), cf(LANE), 0.5 - STEP * SLOT0, -STEP)
        plus(cf(TH1), cf(LANE), 0.5 - STEP * (SLOT0 + 1), -STEP)
    else:
        plus(cf(MINE), cf(LANE), STEP * SLOT0, STEP)
    for k in (2, 1, 3):
        act(unwritten(k), v("m16", 0, 192), F.Copy, scale=0.0)
    plus(v("pois"), v("hold"), -BIG, -2.0)
    act(v("dg"), v("dif"), F.Abs, bias=cf(GRP))
    plus(cf(LHALF), cf(LANE), 0.5)
    act(v("dif"), v("dg"), F.Sign, bias=8.0, scale=-1.0)
    act(v("su"), by(v("su0"), v("uo")), F.Copy)
    for s in range(4):
        act(v("zb", s, 512, 4), v("dif"), F.Relu)
    act(cf(LG0), cf(LANE), F.Relu, bias=-0.625, scale=0.125)
    plus(cf(PFAR), cf(PAR), 0.0, -FAR)
    plus(v("kk"), v("k0", 0, 4), cf(LHALF))
    plus(col(LG), cf(LANE), cf(LG0), 0.125)

    def more_constants():
        plus(v("pay"), v("pay0"), cf(TQ))
        act(v("cross"), v("d2"), F.Abs, bias=cf(PFAR), scale=FAR)
        act(v("ab"), v("m4"), F.Abs, bias=cf(LQ), scale=-1.0)
        act(v("keep4"), v("m4"), F.Sign)
        act(v("pick4"), v("ab"), F.Relu, bias=1.0, scale=-1.0)
        plus(v("pad"), v("pad0"), cf(TQ))
        keys(0)

    def slot(c, n0, n1):
        k, s = SLOT[c]
        return v("tl", 4 * (TOFF[k] + n0) + s, 4 * (TOFF[k] + n1), 4)

    def score(c):
        return v("scn", 16 * c + 15, 16 * c + 16)

    def rsum(c):
        return v("rs", c, c + 1)

    def tile_sum(ks, stop):
        lo, hi = TOFF[ks[0]], TOFF[ks[-1]] + TW[ks[-1]]
        quant("qc", "sc", lo, hi, v("tl", 4 * lo, 4 * hi))
        for k in ks:
            mx(2, QO, ("qc", "sc", TOFF[k], TOFF[k] + TW[k]), k == 0, stop and k == ks[-1])

    def layer(bank0, q, s, tile):
        quant(q, s, 0, 128, v(tile))
        for b in range(4):
            mx(bank0 + b, ("qw", "sw", 128 * b, 128 * b + 128), (q, s, 0, 128))

    def unpack(q, s, which):
        for b in which:
            mx(4 + b, ("qe", "se", 128 * b, 128 * b + 128), (q, s, 0, C))

    def copy_d(name, b):
        act(v(name, b, 4 * C, 4), v("p%d" % (4 + b), 0, C), F.Copy)

    q1, q2, r2, rk = v("er", 15, C, 16), v("rr", 0, 25), v("rr", 32, 57), v("rk", 0, 25)
    top = v("srt", 0, B)

    def slots(step):
        if step == 0:
            ts(v("lc", 32, 57), r2, B - 0.5, cf(LNEW), A.is_lt, A.mult)
        else:
            tt(v("lc", 0, 25), v("lc", 0, 25), v("lc", 32, 57), A.max)

    def places(t):
        qx, sx = "qx%d" % t, "sx%d" % t

        def rest():
            quant_x(t, HEAD, C)
            if EARLY:
                send(raw(v("qr%d" % t)), raw(v(qx)), "arr%d" % t)
                send(v("sr%d" % t), v(sx), "arr%d" % t)
            mx(2, QU, (qx, sx, HEAD, C))
            mx(0, QU, (qx, sx, 0, C))
            mx(1, QU, (qx, sx, 0, 16 * max(ON_S)))

        mx(3, QU, (qx, sx, 0, HEAD))
        rest()
        if t == 0:
            late_fills()
        tt(v("rowp", 0, HEAD), v("p3", 0, HEAD), v("pois", 0, HEAD), A.min)
        scan(v("scn", 0, HEAD), v("hold", 0, HEAD), v("rowp", 0, HEAD), 0.0, A.add, A.max)
        unpack(qx, sx, range(4))
        tt(v("rowp", HEAD, C), v("p2", 0, C - HEAD), v("pois", HEAD, C), A.min)
        if t == 0:
            quant("qo", "so", 0, 128, v("zb"))
        scan(v("scn", HEAD, C), v("hold", HEAD, C), v("rowp", HEAD, C), 0.0, A.add, A.max)

        jobs = [(0, 16, 32), (1, 0, 16)] + [(c, 0, 16 * c) for c in ON_S]

        def sign(i):
            c, lo, hi = jobs[i]
            act(v("sg%d" % (i % 4), 0, hi - lo), v("p3" if c < HEAD // 16 else "p1", lo, hi), F.Sign, bias=score(c), scale=-1.0)

        def positive(i):
            c, lo, hi = jobs[i]
            sg = v("sg%d" % (i % 4), 0, hi - lo)
            if c == 0:
                act(v("ab", 0, 16), sg, F.Sign, bias=1.0, total=rsum(c))
            else:
                act(v("ab", 16, 32) if c == 1 else slot(c, lo, hi), sg, F.Relu, total=rsum(c))

        sign(0)
        for i in range(len(jobs)):
            if i + 1 < len(jobs):
                sign(i + 1)
            positive(i)
        if t == 0:
            more_constants()
        for b in range(4):
            copy_d("dx", b)

        eo = slot("E", 0, C)
        tt(eo, v("scn"), v("p0", 0, C), A.is_ge)
        tiles = [c for c in V_PLAN if isinstance(c, str) and c[0] == "q"]
        for c in V_PLAN:
            if c == "er":
                scan(v("er"), v("kq"), eo, -2048.0, A.max, A.subtract)
            elif c in tiles:
                tile_sum([int(k) for k in c[1:]], c == tiles[-1])
            elif c > 0:
                ts(slot(c, 0, 16 * c), v("p0", 0, 16 * c), score(c), None, A.is_lt)
            else:
                e = 192 * (1 - c - V_LO)
                scan(v("rh", e + 8 * c, e), slot(-c, 0, -8 * c), slot(-c, -8 * c, -16 * c), -128.0, A.add, A.add)
        if EARLY:
            landed([v("qr%d" % t), v("sr%d" % t)], "arr%d" % t, 2 * n_in)
        tt(q2, q1, v("rs", 0, 25), A.subtract)
        tt(v("mm"), v("p2", 0, C), v("pick16"), A.mult)
        tt(v("rr", V_LO, 25), v("rr", V_LO, 25), v("rh", 191, 192 * (25 - V_LO), 192), A.subtract)
        scan(v("dd"), v("keep16"), v("mm"), 0.0, A.min, A.add)
        tt(r2, v("dd", 15, C, 16), q2, A.add)
        cp(rk, r2)
        cp(by(v("srt", 0, C), rk), v("pay"))

    def behind(t):
        nk, nv, cut, last = NK[t], KN["nv"][t], KN["cut"], t + 1 == R
        n4, w, lo = 4 * nk, 16 * nk, 16 * nv
        gl, gr, off, xs = v("gl%d" % t, 0, n4), v("gr%d" % t, 0, n4), v("off", 0, n4), v("xs", 3, w, 4)
        hm = [v("hm", 16 * k, 16 * k + n4) for k in range(3)]

        def search_s():
            for k in range(nv, nk):
                act(v("sg%d" % (k % 2), lo, 320 + w), v("cnt", lo, 320 + w), F.Sign, bias=v("kk", k, k + 1), scale=-1.0,
                    total=v("pb", 168 * k + 167, 168 * k + 168))

        def below():
            for k in range(nv):
                ts(v("le", 336 * k, 336 * k + 336), v("cnt", 16 * k, 16 * k + 336), v("kk", k, k + 1), 2.0, A.is_lt, A.mult)

        def search_v():
            for k in range(nv):
                scan(v("pb", 168 * k, 168 * k + 168), v("le", 336 * k, 336 * k + 168), v("le", 336 * k + 168, 336 * k + 336),
                     32.0 * k - 320.0 - w - lo, A.add, A.add)

        def send_list():
            ts(gl, xs, col(VV), None, A.subtract)
            send(gr, gl, "lst%d" % t)
            landed([gr], "lst%d" % t, n_in)

        def shared(out, win, lst, on_v):
            if on_v < n4:
                act(v(out, 16 * on_v, 4 * w), by(v(win), v(lst, on_v, n4)), F.Copy)
            if on_v:
                cp(v(out, 0, 16 * on_v), by(v(win), v(lst, 0, on_v)))

        def scaled(name, first, n, bank0):
            for b in range(4):
                act(v(name, first + b, first + 4 * n, 4), v("p%d" % (bank0 + b), 0, n), F.Copy, scale=0.03125)

        due, due_t = list(range(4)), list(range(4))
        qt, sq, ns = "qr%d" % t, "sr%d" % t, NS[t]
        cs, cl = (None, None) if EARLY else (v("cs%d" % t, 0, 1), v("cl%d" % t, 0, 1))

        def send_count():
            plus(cs, col(VM2), 0.0, -FINE)
            send(cl, cs, "lst%d" % t)
            landed([cl], "lst%d" % t, n_in)

        def send_s():
            qs, ss = "qs%d" % t, "ss%d" % t
            quant(qs, ss, 0, 128, v("sb"))
            send(raw(v(qt, 128, 128 + ns)), raw(v(qs, 0, ns)), "arr%d" % t)
            send(v(sq, 128, 128 + ns), v(ss, 0, ns), "arr%d" % t)
            landed([v(qt, 128, 128 + ns), v(sq, 128, 128 + ns)], "arr%d" % t, 2 * n_in)

        def h2():
            for b in range(4):
                mx(4 + b, ("qw", "sw", 128 * b, 128 * b + 128), (qt, sq, ns, 128 + ns))
            for b in range(4):
                act(v("sb", 256 + b, 256 + 4 * ns, 4), v("p%d" % (4 + b), 128 - ns, 128), F.Copy, scale=0.03125)

        def put_y(a, b):
            if a < b:
                cp(by(v("st"), v("to", a, b)), v("yt", 16 * a, 16 * b))

        def relabel():
            plus(col(VF), col(VM2), 0.0, -FINE)
            plus(col(KEY1), col(KEY2), col(W2))
            plus(col(LGF), col(LG), (6 + 2 * t) / 8.0, -1.0)
            act(col(KEY1), col(KEY1), F.Abs, bias=col(VF), scale=FINE)
            plus(col(CNT), col(CNT), col(W2))
            act(col(ISV), col(KEY1), F.Relu, bias=1.0, scale=-1.0)
            act(col(LG), col(ISV), F.Identity, bias=col(LG), scale=col(LGF))

        def late():
            if t == 0:
                if EARLY:
                    plus(v("dum"), v("own"), cf(LANE))
                else:
                    plus(v("dum"), v("k0", 0, 16), cf(LANE))
                    plus(cf(LNEW), cf(LQ), 1.5, 2.0)
                    plus(v("kc2"), v("k0", 0, 16), cf(LNEW), 0.5)
                plus(cf(PAR16), cf(PAR), 0.0, 16.0)
                plus(v("lc", 0, 25), v("lc", 32, 57), cf(PAR16))
            plus(cf(LNEW), cf(PAR), 5.0 + t, 16.0)

        def ends():
            if last:
                quant("qv", "sv", 0, 128, v("vb"))
                cp(v("lu", 0, 25), v("lc", 0, 25))

        def new_top():
            if last:
                relabel()
                plus(v("tb", 0, 32), v("cross"), col(LG), 0.0)
            else:
                plus(top, g80, STEP * (SLOT0 + 5 + t))

        def following():
            if last:
                act(v("lf"), by(v("tb", 32, 64), v("lu", 0, 25)), F.Copy, scale=8.0)
                store("a", T.ob[:], (T.lf[0:128:16, :], v("lf")[1]))
            else:
                quant_x(t + 1, 0, HEAD)
                relabel()
                keys(t + 1)

        steps = {
            "lab": lambda: plus(v("lab"), v("srt", B, C), -800.0 / FINE, 1.0 / FINE),
            "lt": lambda: ts(v("lt"), top, -800.0, None, A.add),
            "eq": lambda: ts(v("le", 0, B), v("lt"), cf(MINE), -2.0, A.is_equal, A.mult),
            "written": lambda: red(col(W2), v("le", 0, B), A.add),
            "kr": lambda: ts(v("kr"), v("base"), col(W2), None, A.add),
            "turn": lambda: turn(v("kt"), v("kr")),
            "vm2": lambda: red(col(VM2), v("kt", 32, 64), A.min),
            "vm1": lambda: red(col(VM1), v("kt", 0, 32), A.min),
            "vv": lambda: ts(col(VV), col(VM1), col(VM2), FINE, A.subtract, A.mult),
            "pad": lambda: plus(v("srt", C, C + w), v("pad", 0, w), col(VV)),
            "ind": lambda: ts(v("ind", 0, 320), v("lab"), col(VM2), col(VM1), A.add, A.is_equal),
            "cnt": lambda: scan(v("cnt", 0, 320 + w), v("ind", 0, 320 + w), v("ind", 0, 320 + w), 0.0, A.add, A.max),
            "search_s": search_s, "below": below, "search_v": search_v,
            "pos": lambda: ts(v("pos", 0, nk), v("pb", 167, 168 * nk, 168), 0.5, 240.0 + (w + lo) / 2, A.mult, A.add),
            "xg": lambda: tt(v("xg", 0, w), by(v("srt", 0, C + w), v("pos", 0, nk)), v("pick4", 0, w), A.mult),
            "xs": lambda: scan(v("xs", 0, w), v("keep4", 0, w), v("xg", 0, w), 0.0, A.mult, A.add),
            "gl": send_list,
            "g80": lambda: tt(g80, top, v("lt"), A.subtract),
            "h80": lambda: tt(h80, g80, v("pick4"), A.mult),
            "i80": lambda: scan(i80, v("keep4"), h80, 0.0, A.mult, A.add),
            "to": lambda: cp(v("to"), v("w80", 2 * B + 3, 3 * B, 4)),
            "take_t": lambda: act(v("tt", 0, 4 * B), by(pages(0, C), v("to")), F.Copy),
            "quant_t": lambda: layer(0, "qt", "sq", "tt"),
            "y": lambda: scaled("yt", 0, B, 0),
            "put_y": lambda: put_y(0, cut), "rest_y": lambda: put_y(cut, 20),
            "u": lambda: unpack("qr%d" % t, "sr%d" % t, [due_t.pop(0)]), "d": lambda: due and copy_d("dy", due.pop(0)),
            "e": lambda: t > 0 and copy_d("dy", due.pop(0)),
            "dv": lambda: due and cp(v("dy", due[0], 4 * C, 4), v("p%d" % (4 + due.pop(0)), 0, C)),
            "s0": lambda: act(v("sg0", 0, B), top, F.Sign, bias=cf(TH0), total=col(S0)),
            "s1": lambda: act(v("sg1", 0, B), top, F.Sign, bias=cf(TH1), total=col(S1)),
            "kr2": lambda: ts(v("kr"), v("base"), col(S0), col(S1), A.subtract, A.add),
            "w2": lambda: plus(col(W2), col(S0), col(S1), -1.0),
            "krs": lambda: plus(v("kr"), v("base"), col(W2)),
            "slot0": lambda: slots(0), "slot1": lambda: slots(1),
            "off": lambda: plus(off, v("dum", 0, n4), col(VV)),
            "top": new_top, "pay": lambda: last or act(v("pay"), by(v("srt", 0, C), rk), F.Copy),
            "take_s": lambda: shared("sb", "dy", "gr%d" % t, KN["sv"] * 2 * nk),
            "quant_s": lambda: layer(4, "qs", "ss", "sb"),
            "hm0": lambda: ts(hm[0], gr, SPARE - 0.5, 1e6, A.is_lt, A.mult),
            "hm1": lambda: tt(hm[1], hm[0], off, A.min),
            "hm2": lambda: tt(hm[2], hm[1], xs, A.max),
            "hl": lambda: ts(v("hl", 0, n4), hm[2], col(VV), None, A.subtract),
            "h": lambda: scaled("dx", HO, w, 4),
            "take_z": lambda: shared("zt", "dx", "hl", KN["zv"] * 2 * nk),
            "put_z": lambda: cp(by(v("st"), gl), v("zt", 0, 4 * w)),
            "labels": lambda: last and turn(v("tb", 32, 64), v("tb", 0, 32)),
            "cs": send_count, "vv2": lambda: plus(col(VV), col(VM1), cs, FINE),
            "gl2": lambda: ts(gl, xs, col(VV), None, A.subtract),
            "take_s2": lambda: shared("sb", "dx", "gl%d" % t, KN["sv"] * 2 * nk),
            "send_s": send_s,
            "quant_t2": lambda: layer(0, qt, sq, "tt"),
            "hs0": lambda: act(hm[0], v("kc2", 0, n4), F.Sign, bias=cl, scale=FINE),
            "hs1": lambda: plus(hm[1], hm[0], 128.0, -128.0),
            "hs2": lambda: tt(hm[2], hm[1], v("dum", 0, n4), A.add),
            "hs3": lambda: cp(v("hl", 0, n4), hm[2]),
            "h2": h2,
            "take_z2": lambda: shared("zt", "sb", "hl", KN["zv"] * 2 * nk),
            "late": late, "ends": ends, "next": following}
        done = set()
        for name in PLAN:
            if name[-1] == "'":
                if t > 0:
                    done.add(name[:-1])
                    steps[name[:-1]]()
            elif name not in done:
                steps[name]()

    for t in range(R):
        places(t)
        behind(t)

    qx, sx = "qx%d" % R, "sx%d" % R
    for k, (lo, hi) in enumerate(PIECES):
        quant_x(R, lo, hi)
        mx(k, QV, (qx, sx, lo, hi))
    for k, (lo, hi) in enumerate(PIECES):
        store("s", T.oc[:, 4 * lo:4 * hi], raw(v(qx, lo, hi)))
        if k > 0:
            cp(v("yb", lo, hi), v("p%d" % k, 0, hi - lo))
        else:
            act(v("yb", lo, hi), v("p%d" % k, 0, hi - lo), F.Copy)
        store("a", T.y[:, lo:hi], v("yb", lo, hi))
    for k in range(4):
        store("s", T.osc[4 * k:4 * k + 4, :], (T[sx][32 * k:32 * k + 4, :], v(sx)[1]))
    for sem in SEMAPHORES:
        if sem in count:
            g.wait_ge(T.sem[sem], count[sem])
